import numpy as np
import ml_dtypes


def mxq(x, axis, fmt="e4m3"):
    dtype, down = {"e4m3": (ml_dtypes.float8_e4m3fn, 7), "e5m2": (ml_dtypes.float8_e5m2, 14)}[fmt]
    v = np.moveaxis(np.asarray(x, np.float32).astype(ml_dtypes.bfloat16).astype(np.float64), axis, -1)
    blocks = v.reshape(v.shape[:-1] + (-1, 32))
    amax = np.abs(blocks).max(-1, keepdims=True)
    byte = np.maximum(np.where(amax > 0, np.frexp(amax)[1] - 1 + 127, 0) - down, 1)
    scale = np.exp2(byte - 127.0)
    codes = (blocks / scale).astype(np.float32).astype(dtype).astype(np.float64)
    return np.moveaxis((codes * scale).reshape(v.shape), -1, axis)


WIDE = False


def mx_kscale(k):
    if not WIDE:
        return np.ones(k)
    levels = np.array([10, -10, 5, -5, 0])
    if k % 512:
        return np.exp2(np.random.permutation(np.resize(levels, k // 32))).repeat(32)
    a = np.empty((k // 512, 16))
    for p in range(k // 512):
        a[p, :8] = np.random.permutation(np.resize(levels, 8))
        for g in range(8):
            far = levels[np.abs(levels - a[p, g]) >= 10]
            a[p, g + 8] = far[np.random.randint(len(far))]
    return np.exp2(a.ravel()).repeat(32)


BF16 = ml_dtypes.bfloat16


def bf(x):
    return np.asarray(x, np.float32).astype(BF16)


def f64(x):
    return np.asarray(x).astype(np.float64)


E2M1 = np.array([0.0, 0.5, 1.0, 1.5, 2.0, 3.0, 4.0, 6.0, -0.0, -0.5, -1.0, -1.5, -2.0, -3.0, -4.0, -6.0])


def pack_weight(w, fmt):
    k, n = w.shape
    w = f64(bf(w)).reshape(k // 32, 32, n)
    amax = np.abs(w).max(1)
    if fmt == "e4m3":
        byte = np.frexp(amax)[1] - 1 + 127 - 7
    else:
        mant, ex = np.frexp(amax / 6.0)
        byte = np.where(mant > 0.5, ex, ex - 1) + 127
    byte = np.clip(np.where(amax > 0, byte, 1), 1, 254)
    scaled = (w * np.exp2(127.0 - byte)[:, None, :]).reshape(k, n).astype(np.float32)
    by_word = np.ascontiguousarray(scaled.reshape(k // 512, 128, 4, n).transpose(0, 1, 3, 2))
    if fmt == "e4m3":
        words = by_word.astype(ml_dtypes.float8_e4m3fn).view(np.uint8)
    else:
        c = by_word.astype(ml_dtypes.float4_e2m1fn).view(np.uint8) & 0xF
        words = c[..., 0::2] | (c[..., 1::2] << 4)
    return np.ascontiguousarray(words), np.ascontiguousarray(byte.astype(np.uint8).reshape(k // 512, 16, n))


def unpack_weight(words, scales, fmt):
    g, p, n, _ = words.shape
    if fmt == "e4m3":
        vals = np.ascontiguousarray(words).view(ml_dtypes.float8_e4m3fn).astype(np.float64)
    else:
        nib = np.empty((g, p, n, 4), np.uint8)
        nib[..., 0::2] = words & 0xF
        nib[..., 1::2] = words >> 4
        vals = E2M1[nib]
    vals = vals * np.repeat(np.exp2(scales.astype(np.float64) - 127.0), 8, axis=1)[..., None]
    return vals.transpose(0, 1, 3, 2).reshape(g * 512, n)
def pack4(w):
    words, scales = pack_weight(w, "e2m1")
    return words.reshape(words.shape[0], 128, -1), scales


def unpack4(words, scales):
    return unpack_weight(words.reshape(words.shape[0], 128, -1, 2), scales, "e2m1")


B, D, F, K = 1024, 512, 1024, 2


def draw0():
    u, t = mx_kscale(D), mx_kscale(F)
    inputs = {
        "x": bf(np.random.standard_normal((B, D)) * u),
        "cs": bf(np.random.standard_normal((K, D, F)) / np.sqrt(D) / u[None, :, None]),
        "ss": bf(np.random.standard_normal((K, D, F)) / np.sqrt(D) / u[None, :, None]),
        "gamma": bf(np.random.uniform(0.5, 1.5, (K, F))),
        "g": bf((1.0 + 0.1 * np.random.standard_normal(F)) * t),
    }
    words, scales = pack4(np.random.standard_normal((F, D)) / np.sqrt(F) / t[:, None])
    inputs["dv_words"] = words
    inputs["dv_scales"] = scales
    return inputs


def weno_alpha(s, gamma_k):
    d = 0.5 + s * s
    return gamma_k / (d * d)


def burgers_flux(qh):
    return qh + 0.5 * qh * qh


def core(x, cs, ss, gamma, g, dv_words, dv_scales):
    cs, ss, gamma, g = f64(cs), f64(ss), f64(gamma), f64(g)
    xq = mxq(f64(x), 1, "e4m3")
    q = [(xq @ mxq(cs[k], 0, "e4m3")) for k in range(K)]
    s = [(xq @ mxq(ss[k], 0, "e4m3")) for k in range(K)]
    al = [weno_alpha(s[k], gamma[k][None, :]) for k in range(K)]
    qh = (al[0] * q[0] + al[1] * q[1]) / (al[0] + al[1])
    phi = burgers_flux(qh)
    pg = phi * g[None, :]
    return mxq(pg, 1, "e4m3") @ unpack4(dv_words, dv_scales)


def e4m3fn_bytes(y):
    return np.clip(np.asarray(y, np.float64), -448.0, 448.0).astype(np.float32).astype(ml_dtypes.float8_e4m3fn).view(np.uint8)


def e4m3fn_values(b):
    return np.asarray(b, np.uint8).view(ml_dtypes.float8_e4m3fn).astype(np.float64)


def setup_inputs():
    d = draw0()
    x0 = np.asarray(d['ss']).astype(np.float64)
    s = (np.max(np.abs(x0), axis=(0, 2), keepdims=True) / 448.0).astype(np.float32)
    out = {}
    for k, v in d.items():
        if k == 'ss':
            out['ss_bytes'] = e4m3fn_bytes(x0 / s.astype(np.float64))
            out['ss_scale'] = s
        else:
            out[k] = v
    return out


def reference(x, cs, ss_bytes, ss_scale, gamma, g, dv_words, dv_scales):
    return core(x, cs, e4m3fn_values(ss_bytes) * ss_scale.astype(np.float64), gamma, g, dv_words, dv_scales)

@@ -1,0 +1,428 @@
+from contextlib import ExitStack
+
+import concourse.mybir as mybir
+from concourse.masks import make_identity
+
+F32 = mybir.dt.float32
+BF16 = mybir.dt.bfloat16
+I32 = mybir.dt.int32
+U32 = mybir.dt.uint32
+U8 = mybir.dt.uint8
+FP8 = mybir.dt.float8_e4m3fn
+FP8X4 = mybir.dt.float8_e4m3fn_x4
+FP4X4 = mybir.dt.float4_e2m1fn_x4
+
+ACT = mybir.ActivationFunctionType
+ALU = mybir.AluOpType
+
+P = 128
+PACK = 4
+B, D, F, K = 1024, 512, 1024, 2
+G = 2
+T = 4
+W = 512
+C = 256
+N = 16
+FLOPS = 2 * B * D * F * 2 * K + 2 * B * F * D
+
+CHUNKS = [8,5,3]
+PREP = [3,1,1,1,4,6,6,6,6,1,0,1,4,3,2,6]
+RATE = [0,0,0,0,0,0,0,0,3,1,1,0,0,1,2,0]
+WRATE = [1,0,0,0,1,0,0,1,0,0,0,0,2,1,0,2]
+LAG = 2
+Z_GPSIMD = []
+HELP = []
+OUT_SCALAR = [[9,0],[9,1],[11,0],[11,1],[13,0],[13,1],[15,1]]
+PREP_ITEMS = [["x",1,0],["wd",1,1],["il","c",0,0,1],["qx",1,0],["x",1,1],["qx",1,1],["il","c",1,0,0],["wd",0,1],["il","c",1,0,1],["il","c",0,0,0],["il","c",0,1,0],["il","s",0,1,0],["q","c",0,1,0],["q","c",1,0,1],["q","c",0,0,1],["q","c",0,0,0],["il","s",1,1,0],["q","s",0,1,0],["il","s",1,1,1],["q","s",1,1,0],["il","s",0,1,1],["il","c",0,1,1],["il","c",1,1,1],["q","s",1,1,1],["il","c",1,1,0],["q","s",0,1,1],["q","c",1,0,0],["q","c",0,1,1],["q","c",1,1,1],["q","c",1,1,0]]
+B_ENG = ["G","G","G","G","G","G","G","G","G","G","G","G","G","G","G","G"]
+
+
+def tile_learnedstencilwenostep_w4_kernel(tc, x, cs, ss_bytes, ss_scale, gamma, g, dv_words, dv_scales, out):
+    nc = tc.nc
+    with ExitStack() as ctx:
+        const = ctx.enter_context(tc.tile_pool(name="const", bufs=1))
+        work = ctx.enter_context(tc.tile_pool(name="work", bufs=2))
+        psum = ctx.enter_context(tc.psum_pool(name="psum", bufs=1))
+        ctx.enter_context(tc.manual_schedule())
+
+        sc_t = const.tile([P, PACK], F32, name="sc_t")
+        nc.scalar.dma_start(out=sc_t[:], in_=ss_scale.rearrange("o (p j) u -> p (o j u)", j=PACK))
+        gam_t = []
+        for k in range(K):
+            tl = const.tile([P, G, T], BF16, name="gam_t%d" % k)
+            nc.scalar.dma_start(out=tl[:], in_=gamma[k, :].rearrange("(g p t) -> p g t", g=G, t=T))
+            gam_t.append(tl)
+        g_t = const.tile([P, G, T], BF16, name="g_t")
+        nc.scalar.dma_start(out=g_t[:], in_=g.rearrange("(g p t) -> p g t", g=G, t=T))
+
+        ss_raw = {}
+        cs_raw = {}
+        x_raw = {}
+
+        def load_ss(k, gi):
+            tl = const.tile([P, PACK, W], U8, name="ss_raw%d%d" % (k, gi))
+            nc.sync.dma_start(out=tl[:], in_=ss_bytes[k].rearrange("(p j) f -> p j f", j=PACK)[:, :, gi * W : (gi + 1) * W])
+            ss_raw[k, gi] = tl
+
+        def load_cs(k, gi):
+            tl = const.tile([P, PACK, W], BF16, name="cs_raw%d%d" % (k, gi))
+            nc.sync.dma_start(out=tl[:], in_=cs[k].rearrange("(p j) f -> p j f", j=PACK)[:, :, gi * W : (gi + 1) * W])
+            cs_raw[k, gi] = tl
+
+        def load_x(h, c):
+            tl = const.tile([P, 2, D], BF16, name="x_raw%d%d" % (h, c))
+            nc.sync.dma_start(out=tl[:], in_=x[h * W : (h + 1) * W, :].rearrange("(p r) d -> p r d", r=4)[:, 2 * c : 2 * c + 2, :])
+            x_raw[h, c] = tl
+
+        load_ss(0, 0)
+        load_x(0, 0)
+        load_ss(1, 0)
+        load_x(0, 1)
+        load_cs(0, 0)
+        load_x(1, 0)
+        load_x(1, 1)
+        load_cs(1, 0)
+        load_ss(0, 1)
+        load_ss(1, 1)
+        load_cs(0, 1)
+        load_cs(1, 1)
+        dvw = const.tile([P, G, 2 * D], U8, name="dvw", align_bytes=64)
+        nc.sync.dma_start(out=dvw[:], in_=dv_words.rearrange("g p c -> p g c"))
+        dvs = const.tile([P, G, D], U8, name="dvs", align_bytes=64)
+        nc.gpsimd.memset(dvs[:].rearrange("p g d -> p (g d)").bitcast(I32), 0)
+        for q in range(4):
+            nc.sync.dma_start(
+                out=dvs[32 * q : 32 * q + 4, :, :].bitcast(I32),
+                in_=dv_scales[:, 4 * q : 4 * q + 4, :].rearrange("g q d -> q g d").bitcast(I32),
+            )
+
+        half = const.tile([P, 1], F32, name="half")
+        nc.gpsimd.memset(half[:], 0.5)
+        ident = const.tile([P, P], F32, name="ident")
+        make_identity(nc, ident[:])
+        junk = const.tile([P, 1], F32, name="junk")
+        nc.scalar.activation(out=junk[:], in_=half[:], func=ACT.Ln, bias=half[:, 0:1])
+
+        codes, grouped, wide, xt = {}, {}, {}, {}
+
+        def new_codes(name):
+            c = const.tile([P, C], U32, name="c_" + name, align_bytes=64)
+            s = const.tile([P, C], U8, name="s_" + name, align_bytes=64)
+            return c, s
+
+        def new_grouped():
+            return work.tile([P, PACK * C], BF16, name="grp", bufs=8, align_bytes=64)
+
+        def widen(k, gi, js, on_scalar):
+            if (k, gi) not in wide:
+                wide[k, gi] = work.tile([P, PACK, W], BF16, name="wide", bufs=2)
+            for j in js:
+                src = ss_raw[k, gi][:, j, :].bitcast(FP8)
+                dst = wide[k, gi][:, j, :]
+                if on_scalar:
+                    nc.scalar.activation(out=dst, in_=src, func=ACT.Copy, scale=sc_t[:, j : j + 1])
+                else:
+                    nc.vector.tensor_scalar(out=dst, in0=src, scalar1=sc_t[:, j : j + 1], scalar2=None, op0=ALU.mult)
+
+        def interleave(kind, k, gi, tp):
+            grp = new_grouped()
+            src = wide[k, gi] if kind == "s" else cs_raw[k, gi]
+            d = grp[:].rearrange("p (t m j) -> p t m j", t=2, j=PACK)
+            s = src[:].rearrange("p j (m t) -> p t m j", t=T)[:, 2 * tp : 2 * tp + 2]
+            if kind == "c" and k == 0:
+                nc.vector.tensor_scalar(out=d, in0=s, scalar1=-1.0, scalar2=None, op0=ALU.mult)
+            else:
+                nc.vector.tensor_copy(out=d, in_=s)
+            grouped[kind, k, gi, tp] = grp
+
+        def quant(*key):
+            c, s = new_codes("%s%d%d%d" % key)
+            nc.vector.quantize_mx(out=c[:].bitcast(FP8X4), scales=s[:], in_=grouped[key][:])
+            codes[key] = (c, s)
+
+        def transpose_x(h, c):
+            bank = psum.tile([P, 2, 2, P], F32, name=("dq", "nq")[c], bufs=2)
+            for r in range(2):
+                words = x_raw[h, c][:, r, :].bitcast(F32)
+                for u in range(2):
+                    nc.tensor.transpose(bank[:, r, u, :], words[:, u::2], ident[:])
+            xt[h, c] = bank
+
+        def copy_x(h, c, on_scalar):
+            grp = new_grouped()
+            dst = grp[:].bitcast(F32).rearrange("p (r n u) -> p r u n", r=2, u=2)
+            dst = grp[:].bitcast(F32).rearrange("p (r n u) -> p r n u", r=2, u=2)
+            src = xt[h, c][:].rearrange("p r u n -> p r n u")
+            if on_scalar:
+                nc.scalar.copy(out=dst, in_=src)
+            else:
+                nc.vector.tensor_copy(out=dst, in_=src)
+            grouped["x", 0, h, c] = grp
+
+        def where(u):
+            return u // 8, u // 4 % 2, u // 2 % 2, u % 2
+
+        def mm1(dst, kind, k, u, start, stop):
+            gi, h, c, tp = where(u)
+            wc, ws = codes[kind, k, gi, tp]
+            xc, xs = codes["x", 0, h, c]
+            cols = slice(dst[0] * P, (dst[0] + 1) * P)
+            nc.tensor.matmul_mx(
+                out=dst[1][:, dst[0], :],
+                lhsT=wc[:, cols].bitcast(FP8X4),
+                lhsT_scale=ws[:, cols],
+                rhs=xc[:].bitcast(FP8X4),
+                rhs_scale=xs[:],
+                start=start,
+                stop=stop,
+            )
+
+        s_t, e_t, l_t, z_t, w_t, dq_t, nq_t, t_t, qh_t, b_t = {}, {}, {}, {}, {}, {}, {}, {}, {}, {}
+
+        def emit_s(u, k):
+            bank = psum.tile([P, 2, C], F32, name="s", bufs=4)
+            for i in range(2):
+                mm1((i, bank), "s", k, u, True, True)
+            s_t[u, k] = bank
+
+        def emit_e(u, k):
+            if u not in e_t:
+                e_t[u] = work.tile([P, K, W], F32, name="e", bufs=4)
+            src = s_t[u, k][:].rearrange("p t n -> p (t n)")
+            if [u, k] in HELP:
+                sc = work.tile([P, W], F32, name="sc", bufs=2)
+                nc.vector.tensor_copy(out=sc[:], in_=src)
+                nc.gpsimd.tensor_tensor(out=e_t[u][:, k, :], in0=sc[:], in1=sc[:], op=ALU.mult)
+            else:
+                nc.scalar.activation(out=e_t[u][:, k, :], in_=src, func=ACT.Square)
+
+        def emit_l(u):
+            l = work.tile([P, K, W], F32, name="l", bufs=4)
+            nc.scalar.activation(out=l[:], in_=e_t[u][:], func=ACT.Ln, bias=half[:, 0:1])
+            l_t[u] = l
+
+        def emit_z(u):
+            z = work.tile([P, W], F32, name="z", bufs=9)
+            eng = nc.gpsimd if u in Z_GPSIMD else nc.vector
+            eng.tensor_tensor(out=z[:], in0=l_t[u][:, 0, :], in1=l_t[u][:, 1, :], op=ALU.subtract)
+            z_t[u] = z
+
+        def emit_w(u):
+            gi, h, c, tp = where(u)
+            w = work.tile([P, W], F32, name="w", bufs=9)
+            for i in range(2):
+                col = gi * T + 2 * tp + i
+                cols = slice(i * C, (i + 1) * C)
+                nc.scalar.activation(out=w[:, cols], in_=z_t[u][:, cols], func=ACT.Sigmoid, scale=2.0, bias=lnr[:, col : col + 1])
+            w_t[u] = w
+
+        def emit_dq(u):
+            dq = psum.tile([P, 2, C], F32, name="dq", bufs=2)
+            nq = psum.tile([P, 2, C], F32, name="nq", bufs=2)
+            for i in range(2):
+                mm1((i, dq), "c", 1, u, True, False)
+                mm1((i, dq), "c", 0, u, False, True)
+            for i in range(2):
+                mm1((i, nq), "c", 0, u, True, True)
+            dq_t[u], nq_t[u] = dq, nq
+
+        def emit_t(u):
+            tt = work.tile([P, W], F32, name="tt", bufs=3)
+            nc.vector.tensor_tensor(out=tt[:], in0=dq_t[u][:].rearrange("p t n -> p (t n)"), in1=w_t[u][:], op=ALU.mult)
+            t_t[u] = tt
+
+        def emit_qh(u):
+            v, tp = u // 2, u % 2
+            if tp == 0:
+                qh_t[v] = work.tile([P, T, C], F32, name="qh", bufs=3)
+                b_t[v] = work.tile([P, T, C], F32, name="bb", bufs=3)
+            nc.vector.tensor_tensor(
+                out=qh_t[v][:, 2 * tp : 2 * tp + 2, :].rearrange("p t n -> p (t n)"),
+                in0=t_t[u][:],
+                in1=nq_t[u][:].rearrange("p t n -> p (t n)"),
+                op=ALU.subtract,
+            )
+
+        def emit_b(u):
+            gi, h, c, tp = where(u)
+            for i in range(2):
+                t = 2 * tp + i
+                col = gi * T + t
+                dst, src = b_t[u // 2][:, t, :], qh_t[u // 2][:, t, :]
+                if B_ENG[u] == "S":
+                    nc.scalar.activation(out=dst, in_=src, func=ACT.Identity, scale=gh[:, col : col + 1], bias=gf[:, col : col + 1])
+                else:
+                    eng = nc.gpsimd if B_ENG[u] == "G" else nc.vector
+                    eng.tensor_scalar(out=dst, in0=src, scalar1=gh[:, col : col + 1], scalar2=gf[:, col : col + 1], op0=ALU.mult, op1=ALU.add)
+
+        def emit_pg(u):
+            v = u // 2
+            pg = work.tile([P, C, T], BF16, name="pg", bufs=3, align_bytes=64)
+            nc.vector.tensor_tensor(
+                out=pg[:].rearrange("p (c i) t -> p c t i", i=4),
+                in0=b_t[v][:].rearrange("p t (c i) -> p c t i", i=4),
+                in1=qh_t[v][:].rearrange("p t (c i) -> p c t i", i=4),
+                op=ALU.mult,
+            )
+            grouped["p", v] = pg
+
+        def emit_qp(u):
+            v = u // 2
+            c, s = new_codes("p%d" % v)
+            nc.vector.quantize_mx(out=c[:].bitcast(FP8X4), scales=s[:], in_=grouped["p", v][:].rearrange("p n t -> p (n t)"))
+            codes["p", v] = (c, s)
+
+        outs = {}
+
+        def emit_m(u, r):
+            v = u // 2
+            bank = psum.tile([P, W], F32, name="s", bufs=4)
+            cols = slice(r * P, (r + 1) * P)
+            for gi in range(G):
+                c, s = codes["p", v - 4 + 4 * gi]
+                nc.tensor.matmul_mx(
+                    out=bank[:],
+                    lhsT=c[:, cols].bitcast(FP8X4),
+                    lhsT_scale=s[:, cols],
+                    rhs=dvw[:, gi, :].bitcast(FP4X4),
+                    rhs_scale=dvs[:, gi, :],
+                    start=(gi == 0),
+                    stop=(gi == G - 1),
+                )
+            outs[u, r] = bank
+
+        def emit_o(u, r):
+            gi, h, c, tp = where(u)
+            o = work.tile([P, D], F32, name="o", bufs=4)
+            if [u, r] in OUT_SCALAR:
+                nc.scalar.copy(out=o[:], in_=outs[u, r][:])
+            else:
+                nc.vector.tensor_copy(out=o[:], in_=outs[u, r][:])
+            nc.sync.dma_start(out=out[h * W : (h + 1) * W, :].rearrange("(p r) d -> p r d", r=4)[:, 2 * c + r, :], in_=o[:])
+
+        lg = [const.tile([P, G * T], F32, name="lg%d" % k) for k in range(K)]
+        lnr = const.tile([P, G * T], F32, name="lnr")
+        gf = const.tile([P, G * T], F32, name="gf")
+        gh = const.tile([P, G * T], F32, name="gh")
+
+        ALL = [0, 1, 2, 3]
+        transpose_x(0, 0)
+        widen(0, 0, [0], False)
+        widen(0, 0, [1], False)
+        widen(0, 0, [2], False)
+        widen(0, 0, [3], False)
+        copy_x(0, 0, True)
+        interleave("s", 0, 0, 0)
+        widen(1, 0, [2], True)
+        widen(1, 0, [3], True)
+        quant("s", 0, 0, 0)
+        interleave("s", 0, 0, 1)
+        quant("x", 0, 0, 0)
+        emit_s(0, 0)
+        emit_e(0, 0)
+        widen(1, 0, [0], False)
+        widen(1, 0, [1], False)
+        quant("s", 0, 0, 1)
+        emit_s(1, 0)
+        emit_e(1, 0)
+        interleave("s", 1, 0, 0)
+        quant("s", 1, 0, 0)
+        emit_s(0, 1)
+        emit_e(0, 1)
+        transpose_x(0, 1)
+        copy_x(0, 1, True)
+        interleave("s", 1, 0, 1)
+        quant("s", 1, 0, 1)
+        emit_s(1, 1)
+        quant("x", 0, 0, 1)
+        HEAD_E = [(0, 0), (1, 0), (0, 1)]
+        for k in range(K):
+            nc.scalar.activation(out=lg[k][:], in_=gam_t[k][:].rearrange("p g t -> p (g t)"), func=ACT.Ln)
+        nc.gpsimd.tensor_tensor(out=lnr[:], in0=lg[1][:], in1=lg[0][:], op=ALU.subtract)
+        nc.gpsimd.tensor_copy(out=gf[:], in_=g_t[:].rearrange("p g t -> p (g t)"))
+        nc.gpsimd.tensor_scalar(out=gh[:], in0=gf[:], scalar1=0.5, scalar2=0.0, op0=ALU.mult, op1=ALU.add)
+
+        items = list(PREP_ITEMS)
+
+        def prep(n):
+            for it in items[:n]:
+                if it[0] == "x":
+                    transpose_x(it[1], it[2])
+                    copy_x(it[1], it[2], False)
+                elif it[0] == "qx":
+                    quant("x", 0, it[1], it[2])
+                elif it[0] == "wd":
+                    widen(it[1], it[2], ALL, False)
+                elif it[0] == "il":
+                    interleave(it[1], it[2], it[3], it[4])
+                else:
+                    quant(it[1], it[2], it[3], it[4])
+            del_n = min(n, len(items))
+            items[:] = items[del_n:]
+
+        state = {"v": 0}
+
+        def dq(v):
+            if v < N and v not in dq_t:
+                emit_dq(v)
+
+        def flux():
+            v = state["v"]
+            dq(v)
+            dq(v + 1)
+            if v < N:
+                emit_t(v)
+            if 1 <= v <= N:
+                emit_qh(v - 1)
+                emit_b(v - 1)
+            w = v - 1 - LAG
+            if 0 <= w < N and w % 2 == 1:
+                emit_pg(w)
+            w = v - 2 - LAG
+            if 0 <= w < N and w % 2 == 1:
+                emit_qp(w)
+                if w >= 8:
+                    for r in range(2):
+                        emit_m(w, r)
+            w = v - 3 - LAG
+            if 8 <= w < N and w % 2 == 1:
+                for r in range(2):
+                    emit_o(w, r)
+            state["v"] = v + 1
+
+        def s(u):
+            for k in range(K):
+                if u < N and (u, k) not in s_t:
+                    emit_s(u, k)
+
+        done = []
+
+        def e(u):
+            for k in range(K):
+                if u < N and (u, k) not in HEAD_E and (u, k) not in done:
+                    done.append((u, k))
+                    emit_e(u, k)
+
+        u = 0
+        for n in CHUNKS:
+            for i in range(u, u + n):
+                prep(PREP[i])
+                s(i)
+                s(i + 1)
+                e(i)
+                e(i + 1)
+                s(i + 2)
+                emit_l(i)
+                if i > u:
+                    emit_z(i - 1)
+                for _ in range(RATE[i]):
+                    flux()
+            emit_z(u + n - 1)
+            for i in range(u, u + n):
+                emit_w(i)
+            for _ in range(sum(WRATE[u : u + n])):
+                flux()
+            u += n
+        prep(99)
+        while state["v"] < N + 4 + LAG:
+            flux()

@@ -25,16 +25,16 @@ C = 256
 N = 16
 FLOPS = 2 * B * D * F * 2 * K + 2 * B * F * D
 
-CHUNKS = [8,5,3]
-PREP = [3,1,1,1,4,6,6,6,6,1,0,1,4,3,2,6]
-RATE = [0,0,0,0,0,0,0,0,3,1,1,0,0,1,2,0]
-WRATE = [1,0,0,0,1,0,0,1,0,0,0,0,2,1,0,2]
+CHUNKS = [9,4,3]
+PREP = [5,2,5,6,3,1,6,0,4,4,4,0,2,4,6,3]
+RATE = [0,0,0,0,0,0,0,0,0,1,1,2,0,2,1,0]
+WRATE = [1,1,0,0,0,1,0,1,0,0,1,0,0,1,1,1]
 LAG = 2
 Z_GPSIMD = []
 HELP = []
 OUT_SCALAR = [[9,0],[9,1],[11,0],[11,1],[13,0],[13,1],[15,1]]
-PREP_ITEMS = [["x",1,0],["wd",1,1],["il","c",0,0,1],["qx",1,0],["x",1,1],["qx",1,1],["il","c",1,0,0],["wd",0,1],["il","c",1,0,1],["il","c",0,0,0],["il","c",0,1,0],["il","s",0,1,0],["q","c",0,1,0],["q","c",1,0,1],["q","c",0,0,1],["q","c",0,0,0],["il","s",1,1,0],["q","s",0,1,0],["il","s",1,1,1],["q","s",1,1,0],["il","s",0,1,1],["il","c",0,1,1],["il","c",1,1,1],["q","s",1,1,1],["il","c",1,1,0],["q","s",0,1,1],["q","c",1,0,0],["q","c",0,1,1],["q","c",1,1,1],["q","c",1,1,0]]
-B_ENG = ["G","G","G","G","G","G","G","G","G","G","G","G","G","G","G","G"]
+PREP_ITEMS = [["x",1,0],["il","c",0,1,1],["il","c",1,0,0],["x",1,1],["il","c",0,0,0],["qx",1,0],["qx",1,1],["wd",1,1],["il","s",1,1,1],["wd",0,1],["il","c",1,0,1],["q","c",0,1,1],["q","c",0,0,0],["il","s",1,1,0],["il","c",0,0,1],["il","s",0,1,1],["il","c",1,1,1],["q","c",1,1,1],["q","s",1,1,0],["il","s",0,1,0],["q","s",0,1,1],["q","s",0,1,0],["q","c",0,0,1],["il","c",0,1,0],["q","s",1,1,1],["il","c",1,1,0],["q","c",0,1,0],["q","c",1,0,0],["q","c",1,1,0],["q","c",1,0,1]]
+B_ENG = ["V","V","V","V","V","S","V","V","V","V","V","S","S","S","S","S"]
 
 
 def tile_learnedstencilwenostep_w4_kernel(tc, x, cs, ss_bytes, ss_scale, gamma, g, dv_words, dv_scales, out):

@@ -25,16 +25,16 @@ C = 256
 N = 16
 FLOPS = 2 * B * D * F * 2 * K + 2 * B * F * D
 
-CHUNKS = [9,4,3]
-PREP = [5,2,5,6,3,1,6,0,4,4,4,0,2,4,6,3]
-RATE = [0,0,0,0,0,0,0,0,0,1,1,2,0,2,1,0]
-WRATE = [1,1,0,0,0,1,0,1,0,0,1,0,0,1,1,1]
-LAG = 2
+CHUNKS = [10,6]
+PREP = [4,3,1,2,6,4,3,6,6,3,4,6,4,4,0,3]
+RATE = [0,0,0,0,0,0,0,0,0,0,1,1,1,2,0,0]
+WRATE = [0,2,0,1,2,0,0,0,0,0,2,0,3,3,0,1]
+LAG = 1
 Z_GPSIMD = []
 HELP = []
 OUT_SCALAR = [[9,0],[9,1],[11,0],[11,1],[13,0],[13,1],[15,1]]
-PREP_ITEMS = [["x",1,0],["il","c",0,1,1],["il","c",1,0,0],["x",1,1],["il","c",0,0,0],["qx",1,0],["qx",1,1],["wd",1,1],["il","s",1,1,1],["wd",0,1],["il","c",1,0,1],["q","c",0,1,1],["q","c",0,0,0],["il","s",1,1,0],["il","c",0,0,1],["il","s",0,1,1],["il","c",1,1,1],["q","c",1,1,1],["q","s",1,1,0],["il","s",0,1,0],["q","s",0,1,1],["q","s",0,1,0],["q","c",0,0,1],["il","c",0,1,0],["q","s",1,1,1],["il","c",1,1,0],["q","c",0,1,0],["q","c",1,0,0],["q","c",1,1,0],["q","c",1,0,1]]
-B_ENG = ["V","V","V","V","V","S","V","V","V","V","V","S","S","S","S","S"]
+PREP_ITEMS = [["x",1,0],["x",1,1],["qx",1,0],["qx",1,1],["wd",0,1],["wd",1,1],["il","s",0,1,0],["il","s",1,1,0],["q","s",0,1,0],["q","s",1,1,0],["il","s",0,1,1],["il","s",1,1,1],["q","s",0,1,1],["q","s",1,1,1],["il","c",0,0,0],["il","c",1,0,0],["q","c",0,0,0],["q","c",1,0,0],["il","c",0,0,1],["il","c",1,0,1],["q","c",0,0,1],["q","c",1,0,1],["il","c",0,1,0],["il","c",1,1,0],["q","c",0,1,0],["q","c",1,1,0],["il","c",0,1,1],["il","c",1,1,1],["q","c",0,1,1],["q","c",1,1,1]]
+B_ENG = ["V","V","V","V","V","V","V","V","S","S","S","S","S","S","S","V"]
 
 
 def tile_learnedstencilwenostep_w4_kernel(tc, x, cs, ss_bytes, ss_scale, gamma, g, dv_words, dv_scales, out):
@@ -78,12 +78,12 @@ def tile_learnedstencilwenostep_w4_kernel(tc, x, cs, ss_bytes, ss_scale, gamma, 
         load_x(0, 0)
         load_ss(1, 0)
         load_x(0, 1)
-        load_cs(0, 0)
         load_x(1, 0)
         load_x(1, 1)
-        load_cs(1, 0)
         load_ss(0, 1)
         load_ss(1, 1)
+        load_cs(0, 0)
+        load_cs(1, 0)
         load_cs(0, 1)
         load_cs(1, 1)
         dvw = const.tile([P, G, 2 * D], U8, name="dvw", align_bytes=64)
@@ -111,7 +111,7 @@ def tile_learnedstencilwenostep_w4_kernel(tc, x, cs, ss_bytes, ss_scale, gamma, 
             return c, s
 
         def new_grouped():
-            return work.tile([P, PACK * C], BF16, name="grp", bufs=8, align_bytes=64)
+            return work.tile([P, PACK * C], BF16, name="grp", bufs=6, align_bytes=64)
 
         def widen(k, gi, js, on_scalar):
             if (k, gi) not in wide:
@@ -202,14 +202,14 @@ def tile_learnedstencilwenostep_w4_kernel(tc, x, cs, ss_bytes, ss_scale, gamma, 
             l_t[u] = l
 
         def emit_z(u):
-            z = work.tile([P, W], F32, name="z", bufs=9)
+            z = work.tile([P, W], F32, name="z", bufs=11)
             eng = nc.gpsimd if u in Z_GPSIMD else nc.vector
             eng.tensor_tensor(out=z[:], in0=l_t[u][:, 0, :], in1=l_t[u][:, 1, :], op=ALU.subtract)
             z_t[u] = z
 
         def emit_w(u):
             gi, h, c, tp = where(u)
-            w = work.tile([P, W], F32, name="w", bufs=9)
+            w = work.tile([P, W], F32, name="w", bufs=11)
             for i in range(2):
                 col = gi * T + 2 * tp + i
                 cols = slice(i * C, (i + 1) * C)
@@ -372,19 +372,20 @@ def tile_learnedstencilwenostep_w4_kernel(tc, x, cs, ss_bytes, ss_scale, gamma, 
             dq(v + 1)
             if v < N:
                 emit_t(v)
+            if 2 <= v <= N + 1:
+                emit_b(v - 2)
             if 1 <= v <= N:
                 emit_qh(v - 1)
-                emit_b(v - 1)
-            w = v - 1 - LAG
+            w = v - 2 - LAG
             if 0 <= w < N and w % 2 == 1:
                 emit_pg(w)
-            w = v - 2 - LAG
+            w = v - 3 - LAG
             if 0 <= w < N and w % 2 == 1:
                 emit_qp(w)
                 if w >= 8:
                     for r in range(2):
                         emit_m(w, r)
-            w = v - 3 - LAG
+            w = v - 4 - LAG
             if 8 <= w < N and w % 2 == 1:
                 for r in range(2):
                     emit_o(w, r)
@@ -424,5 +425,5 @@ def tile_learnedstencilwenostep_w4_kernel(tc, x, cs, ss_bytes, ss_scale, gamma, 
                 flux()
             u += n
         prep(99)
-        while state["v"] < N + 4 + LAG:
+        while state["v"] < N + 5 + LAG:
             flux()

@@ -26,10 +26,10 @@ N = 16
 FLOPS = 2 * B * D * F * 2 * K + 2 * B * F * D
 
 CHUNKS = [10,6]
-PREP = [4,3,1,2,6,4,3,6,6,3,4,6,4,4,0,3]
-RATE = [0,0,0,0,0,0,0,0,0,0,1,1,1,2,0,0]
-WRATE = [0,2,0,1,2,0,0,0,0,0,2,0,3,3,0,1]
-LAG = 1
+PREP = [6,3,3,3,3,3,3,3,3,3,3,3,3,3,3,3]
+RATE = [0,0,0,0,0,0,0,0,0,0,1,1,1,1,1,1]
+WRATE = [4,0,0,0,0,0,0,0,0,0,2,0,0,0,0,0]
+LAG = 0
 Z_GPSIMD = []
 HELP = []
 OUT_SCALAR = [[9,0],[9,1],[11,0],[11,1],[13,0],[13,1],[15,1]]
@@ -47,13 +47,6 @@ def tile_learnedstencilwenostep_w4_kernel(tc, x, cs, ss_bytes, ss_scale, gamma, 
 
         sc_t = const.tile([P, PACK], F32, name="sc_t")
         nc.scalar.dma_start(out=sc_t[:], in_=ss_scale.rearrange("o (p j) u -> p (o j u)", j=PACK))
-        gam_t = []
-        for k in range(K):
-            tl = const.tile([P, G, T], BF16, name="gam_t%d" % k)
-            nc.scalar.dma_start(out=tl[:], in_=gamma[k, :].rearrange("(g p t) -> p g t", g=G, t=T))
-            gam_t.append(tl)
-        g_t = const.tile([P, G, T], BF16, name="g_t")
-        nc.scalar.dma_start(out=g_t[:], in_=g.rearrange("(g p t) -> p g t", g=G, t=T))
 
         ss_raw = {}
         cs_raw = {}
@@ -84,6 +77,13 @@ def tile_learnedstencilwenostep_w4_kernel(tc, x, cs, ss_bytes, ss_scale, gamma, 
         load_ss(1, 1)
         load_cs(0, 0)
         load_cs(1, 0)
+        gam_t = []
+        for k in range(K):
+            tl = const.tile([P, G, T], BF16, name="gam_t%d" % k)
+            nc.sync.dma_start(out=tl[:], in_=gamma[k, :].rearrange("(g p t) -> p g t", g=G, t=T))
+            gam_t.append(tl)
+        g_t = const.tile([P, G, T], BF16, name="g_t")
+        nc.sync.dma_start(out=g_t[:], in_=g.rearrange("(g p t) -> p g t", g=G, t=T))
         load_cs(0, 1)
         load_cs(1, 1)
         dvw = const.tile([P, G, 2 * D], U8, name="dvw", align_bytes=64)
@@ -127,8 +127,8 @@ def tile_learnedstencilwenostep_w4_kernel(tc, x, cs, ss_bytes, ss_scale, gamma, 
         def interleave(kind, k, gi, tp):
             grp = new_grouped()
             src = wide[k, gi] if kind == "s" else cs_raw[k, gi]
-            d = grp[:].rearrange("p (t m j) -> p t m j", t=2, j=PACK)
-            s = src[:].rearrange("p j (m t) -> p t m j", t=T)[:, 2 * tp : 2 * tp + 2]
+            d = grp[:].rearrange("p (t m j) -> p m t j", t=2, j=PACK)
+            s = src[:].rearrange("p j (m t) -> p m t j", t=T)[:, :, 2 * tp : 2 * tp + 2, :]
             if kind == "c" and k == 0:
                 nc.vector.tensor_scalar(out=d, in0=s, scalar1=-1.0, scalar2=None, op0=ALU.mult)
             else:
@@ -255,24 +255,25 @@ def tile_learnedstencilwenostep_w4_kernel(tc, x, cs, ss_bytes, ss_scale, gamma, 
                     eng = nc.gpsimd if B_ENG[u] == "G" else nc.vector
                     eng.tensor_scalar(out=dst, in0=src, scalar1=gh[:, col : col + 1], scalar2=gf[:, col : col + 1], op0=ALU.mult, op1=ALU.add)
 
-        def emit_pg(u):
+        def emit_pg(u, cols):
             v = u // 2
-            pg = work.tile([P, C, T], BF16, name="pg", bufs=3, align_bytes=64)
+            if v not in pg_t:
+                pg_t[v] = work.tile([P, C, T], BF16, name="pg", bufs=3, align_bytes=64)
+                codes["p", v] = new_codes("p%d" % v)
             nc.vector.tensor_tensor(
-                out=pg[:].rearrange("p (c i) t -> p c t i", i=4),
-                in0=b_t[v][:].rearrange("p t (c i) -> p c t i", i=4),
-                in1=qh_t[v][:].rearrange("p t (c i) -> p c t i", i=4),
+                out=pg_t[v][:, cols, :].rearrange("p (c i) t -> p c t i", i=4),
+                in0=b_t[v][:, :, cols].rearrange("p t (c i) -> p c t i", i=4),
+                in1=qh_t[v][:, :, cols].rearrange("p t (c i) -> p c t i", i=4),
                 op=ALU.mult,
             )
-            grouped["p", v] = pg
 
-        def emit_qp(u):
+        def emit_qp(u, cols):
             v = u // 2
-            c, s = new_codes("p%d" % v)
-            nc.vector.quantize_mx(out=c[:].bitcast(FP8X4), scales=s[:], in_=grouped["p", v][:].rearrange("p n t -> p (n t)"))
-            codes["p", v] = (c, s)
+            c, s = codes["p", v]
+            nc.vector.quantize_mx(out=c[:, cols].bitcast(FP8X4), scales=s[:, cols], in_=pg_t[v][:, cols, :].rearrange("p n t -> p (n t)"))
 
         outs = {}
+        pg_t = {}
 
         def emit_m(u, r):
             v = u // 2
@@ -336,11 +337,12 @@ def tile_learnedstencilwenostep_w4_kernel(tc, x, cs, ss_bytes, ss_scale, gamma, 
         emit_s(1, 1)
         quant("x", 0, 0, 1)
         HEAD_E = [(0, 0), (1, 0), (0, 1)]
-        for k in range(K):
-            nc.scalar.activation(out=lg[k][:], in_=gam_t[k][:].rearrange("p g t -> p (g t)"), func=ACT.Ln)
-        nc.gpsimd.tensor_tensor(out=lnr[:], in0=lg[1][:], in1=lg[0][:], op=ALU.subtract)
-        nc.gpsimd.tensor_copy(out=gf[:], in_=g_t[:].rearrange("p g t -> p (g t)"))
-        nc.gpsimd.tensor_scalar(out=gh[:], in0=gf[:], scalar1=0.5, scalar2=0.0, op0=ALU.mult, op1=ALU.add)
+        def channel_constants():
+            for k in range(K):
+                nc.scalar.activation(out=lg[k][:], in_=gam_t[k][:].rearrange("p g t -> p (g t)"), func=ACT.Ln)
+            nc.gpsimd.tensor_tensor(out=lnr[:], in0=lg[1][:], in1=lg[0][:], op=ALU.subtract)
+            nc.gpsimd.tensor_copy(out=gf[:], in_=g_t[:].rearrange("p g t -> p (g t)"))
+            nc.gpsimd.tensor_scalar(out=gh[:], in0=gf[:], scalar1=0.5, scalar2=0.0, op0=ALU.mult, op1=ALU.add)
 
         items = list(PREP_ITEMS)
 
@@ -377,11 +379,17 @@ def tile_learnedstencilwenostep_w4_kernel(tc, x, cs, ss_bytes, ss_scale, gamma, 
             if 1 <= v <= N:
                 emit_qh(v - 1)
             w = v - 2 - LAG
-            if 0 <= w < N and w % 2 == 1:
-                emit_pg(w)
+            if 0 <= w < N - 1 and w % 2 == 1:
+                emit_pg(w, slice(0, C))
+            if w == N - 1:
+                for r in range(2):
+                    emit_pg(w, slice(r * P, (r + 1) * P))
+                for r in range(2):
+                    emit_qp(w, slice(r * P, (r + 1) * P))
+                    emit_m(w, r)
             w = v - 3 - LAG
-            if 0 <= w < N and w % 2 == 1:
-                emit_qp(w)
+            if 0 <= w < N - 1 and w % 2 == 1:
+                emit_qp(w, slice(0, C))
                 if w >= 8:
                     for r in range(2):
                         emit_m(w, r)
@@ -414,6 +422,8 @@ def tile_learnedstencilwenostep_w4_kernel(tc, x, cs, ss_bytes, ss_scale, gamma, 
                 e(i + 1)
                 s(i + 2)
                 emit_l(i)
+                if i == 6:
+                    channel_constants()
                 if i > u:
                     emit_z(i - 1)
                 for _ in range(RATE[i]):

@@ -15,26 +15,25 @@ FP4X4 = mybir.dt.float4_e2m1fn_x4
 ACT = mybir.ActivationFunctionType
 ALU = mybir.AluOpType
 
-P = 128
-PACK = 4
 B, D, F, K = 1024, 512, 1024, 2
-G = 2
-T = 4
-W = 512
-C = 256
-N = 16
 FLOPS = 2 * B * D * F * 2 * K + 2 * B * F * D
 
-CHUNKS = [10,6]
-PREP = [6,3,3,3,3,3,3,3,3,3,3,3,3,3,3,3]
-RATE = [0,0,0,0,0,0,0,0,0,0,1,1,1,1,1,1]
-WRATE = [4,0,0,0,0,0,0,0,0,0,2,0,0,0,0,0]
-LAG = 0
-Z_GPSIMD = []
-HELP = []
-OUT_SCALAR = [[9,0],[9,1],[11,0],[11,1],[13,0],[13,1],[15,1]]
-PREP_ITEMS = [["x",1,0],["x",1,1],["qx",1,0],["qx",1,1],["wd",0,1],["wd",1,1],["il","s",0,1,0],["il","s",1,1,0],["q","s",0,1,0],["q","s",1,1,0],["il","s",0,1,1],["il","s",1,1,1],["q","s",0,1,1],["q","s",1,1,1],["il","c",0,0,0],["il","c",1,0,0],["q","c",0,0,0],["q","c",1,0,0],["il","c",0,0,1],["il","c",1,0,1],["q","c",0,0,1],["q","c",1,0,1],["il","c",0,1,0],["il","c",1,1,0],["q","c",0,1,0],["q","c",1,1,0],["il","c",0,1,1],["il","c",1,1,1],["q","c",0,1,1],["q","c",1,1,1]]
-B_ENG = ["V","V","V","V","V","V","V","V","S","S","S","S","S","S","S","V"]
+P = 128
+PACK = 4
+GROUP = P * PACK
+GROUPS = F // GROUP
+TILES = 4
+QROWS = 256
+QUARTERS = B // QROWS
+RTILES = QROWS // P
+BANK = 512
+
+UNITS = GROUPS * QUARTERS * TILES // 2
+
+CHUNKS = (9, 5, 2)
+FLUX_BEHIND = (4, 2, 0)
+PREP_FIRST, PREP_EACH = 6, 3
+SLOPE_ON_SCALAR = range(9, 15)
 
 
 def tile_learnedstencilwenostep_w4_kernel(tc, x, cs, ss_bytes, ss_scale, gamma, g, dv_words, dv_scales, out):
@@ -45,395 +44,368 @@ def tile_learnedstencilwenostep_w4_kernel(tc, x, cs, ss_bytes, ss_scale, gamma, 
         psum = ctx.enter_context(tc.psum_pool(name="psum", bufs=1))
         ctx.enter_context(tc.manual_schedule())
 
-        sc_t = const.tile([P, PACK], F32, name="sc_t")
-        nc.scalar.dma_start(out=sc_t[:], in_=ss_scale.rearrange("o (p j) u -> p (o j u)", j=PACK))
+        scale_col = const.tile([P, PACK], F32, name="scale_col")
+        nc.scalar.dma_start(out=scale_col[:], in_=ss_scale.rearrange("o (p j) u -> p (o j u)", j=PACK))
 
-        ss_raw = {}
-        cs_raw = {}
-        x_raw = {}
+        ss_rows, cs_rows, x_rows = {}, {}, {}
 
-        def load_ss(k, gi):
-            tl = const.tile([P, PACK, W], U8, name="ss_raw%d%d" % (k, gi))
-            nc.sync.dma_start(out=tl[:], in_=ss_bytes[k].rearrange("(p j) f -> p j f", j=PACK)[:, :, gi * W : (gi + 1) * W])
-            ss_raw[k, gi] = tl
+        def load_weight(rows, name, source, dtype, k, gi):
+            rows[k, gi] = const.tile([P, PACK, GROUP], dtype, name="%s%d%d" % (name, k, gi))
+            cols = slice(gi * GROUP, (gi + 1) * GROUP)
+            nc.sync.dma_start(out=rows[k, gi][:], in_=source[k].rearrange("(p j) f -> p j f", j=PACK)[:, :, cols])
 
-        def load_cs(k, gi):
-            tl = const.tile([P, PACK, W], BF16, name="cs_raw%d%d" % (k, gi))
-            nc.sync.dma_start(out=tl[:], in_=cs[k].rearrange("(p j) f -> p j f", j=PACK)[:, :, gi * W : (gi + 1) * W])
-            cs_raw[k, gi] = tl
+        def load_x(q):
+            x_rows[q] = const.tile([P, RTILES, D], BF16, name="x_rows%d" % q)
+            nc.sync.dma_start(out=x_rows[q][:], in_=x[q * QROWS : (q + 1) * QROWS, :].rearrange("(p r) d -> p r d", r=RTILES))
 
-        def load_x(h, c):
-            tl = const.tile([P, 2, D], BF16, name="x_raw%d%d" % (h, c))
-            nc.sync.dma_start(out=tl[:], in_=x[h * W : (h + 1) * W, :].rearrange("(p r) d -> p r d", r=4)[:, 2 * c : 2 * c + 2, :])
-            x_raw[h, c] = tl
+        def load_channels(vector, name):
+            tile = const.tile([P, GROUPS, TILES], BF16, name=name)
+            nc.sync.dma_start(out=tile[:], in_=vector.rearrange("(g p t) -> p g t", g=GROUPS, t=TILES))
+            return tile[:].rearrange("p g t -> p (g t)")
 
-        load_ss(0, 0)
-        load_x(0, 0)
-        load_ss(1, 0)
-        load_x(0, 1)
-        load_x(1, 0)
-        load_x(1, 1)
-        load_ss(0, 1)
-        load_ss(1, 1)
-        load_cs(0, 0)
-        load_cs(1, 0)
-        gam_t = []
+        load_weight(ss_rows, "ss_rows", ss_bytes, U8, 0, 0)
+        load_x(0)
+        load_weight(ss_rows, "ss_rows", ss_bytes, U8, 1, 0)
+        for q in range(1, QUARTERS):
+            load_x(q)
         for k in range(K):
-            tl = const.tile([P, G, T], BF16, name="gam_t%d" % k)
-            nc.sync.dma_start(out=tl[:], in_=gamma[k, :].rearrange("(g p t) -> p g t", g=G, t=T))
-            gam_t.append(tl)
-        g_t = const.tile([P, G, T], BF16, name="g_t")
-        nc.sync.dma_start(out=g_t[:], in_=g.rearrange("(g p t) -> p g t", g=G, t=T))
-        load_cs(0, 1)
-        load_cs(1, 1)
-        dvw = const.tile([P, G, 2 * D], U8, name="dvw", align_bytes=64)
-        nc.sync.dma_start(out=dvw[:], in_=dv_words.rearrange("g p c -> p g c"))
-        dvs = const.tile([P, G, D], U8, name="dvs", align_bytes=64)
-        nc.gpsimd.memset(dvs[:].rearrange("p g d -> p (g d)").bitcast(I32), 0)
-        for q in range(4):
+            load_weight(ss_rows, "ss_rows", ss_bytes, U8, k, 1)
+        for k in range(K):
+            load_weight(cs_rows, "cs_rows", cs, BF16, k, 0)
+        gamma_bf = [load_channels(gamma[k, :], "gamma_bf%d" % k) for k in range(K)]
+        gain_bf = load_channels(g, "gain_bf")
+        for k in range(K):
+            load_weight(cs_rows, "cs_rows", cs, BF16, k, 1)
+        dv_codes = const.tile([P, GROUPS, 2 * D], U8, name="dv_codes", align_bytes=64)
+        nc.sync.dma_start(out=dv_codes[:], in_=dv_words.rearrange("g p c -> p g c"))
+        dv_plane = const.tile([P, GROUPS, D], U8, name="dv_plane", align_bytes=64)
+        nc.gpsimd.memset(dv_plane[:].rearrange("p g d -> p (g d)").bitcast(I32), 0)
+        for quadrant in range(4):
             nc.sync.dma_start(
-                out=dvs[32 * q : 32 * q + 4, :, :].bitcast(I32),
-                in_=dv_scales[:, 4 * q : 4 * q + 4, :].rearrange("g q d -> q g d").bitcast(I32),
+                out=dv_plane[32 * quadrant : 32 * quadrant + 4, :, :].bitcast(I32),
+                in_=dv_scales[:, 4 * quadrant : 4 * quadrant + 4, :].rearrange("g r d -> r g d").bitcast(I32),
             )
 
         half = const.tile([P, 1], F32, name="half")
         nc.gpsimd.memset(half[:], 0.5)
         ident = const.tile([P, P], F32, name="ident")
         make_identity(nc, ident[:])
-        junk = const.tile([P, 1], F32, name="junk")
-        nc.scalar.activation(out=junk[:], in_=half[:], func=ACT.Ln, bias=half[:, 0:1])
+        zeros = const.tile([P, BANK], BF16, name="zeros")
+        nc.vector.memset(zeros[:], 0.0)
+        unused = const.tile([P, 1], F32, name="unused")
+        nc.scalar.activation(out=unused[:], in_=half[:], func=ACT.Ln, bias=half[:, 0:1])
 
-        codes, grouped, wide, xt = {}, {}, {}, {}
+        log_gamma = [const.tile([P, GROUPS * TILES], F32, name="log_gamma%d" % k) for k in range(K)]
+        log_ratio = const.tile([P, GROUPS * TILES], F32, name="log_ratio")
+        gain = const.tile([P, GROUPS * TILES], F32, name="gain")
+        half_gain = const.tile([P, GROUPS * TILES], F32, name="half_gain")
 
-        def new_codes(name):
-            c = const.tile([P, C], U32, name="c_" + name, align_bytes=64)
-            s = const.tile([P, C], U8, name="s_" + name, align_bytes=64)
-            return c, s
+        def channel_constants():
+            for k in range(K):
+                nc.scalar.activation(out=log_gamma[k][:], in_=gamma_bf[k], func=ACT.Ln)
+            nc.gpsimd.tensor_tensor(out=log_ratio[:], in0=log_gamma[1][:], in1=log_gamma[0][:], op=ALU.subtract)
+            nc.gpsimd.tensor_copy(out=gain[:], in_=gain_bf)
+            nc.gpsimd.tensor_scalar(out=half_gain[:], in0=gain[:], scalar1=0.5, scalar2=0.0, op0=ALU.mult, op1=ALU.add)
 
-        def new_grouped():
-            return work.tile([P, PACK * C], BF16, name="grp", bufs=6, align_bytes=64)
+        def keep_busy(tag, bufs, passes):
+            bank = psum.tile([P, BANK], F32, name=tag, bufs=bufs)
+            for _ in range(passes):
+                nc.tensor.matmul(out=bank[:], lhsT=zeros[:, 0:P], rhs=zeros[:], start=True, stop=True)
 
-        def widen(k, gi, js, on_scalar):
+        wide, grouped, codes, turned = {}, {}, {}, {}
+
+        def new_codes(key, columns):
+            name = "_".join([str(part) for part in key])
+            words = const.tile([P, columns], U32, name="words_" + name, align_bytes=64)
+            plane = const.tile([P, columns], U8, name="plane_" + name, align_bytes=64)
+            codes[key] = (words, plane)
+
+        def quantize(key, source, columns, cols):
+            if key not in codes:
+                new_codes(key, columns)
+            words, plane = codes[key]
+            nc.vector.quantize_mx(out=words[:, cols].bitcast(FP8X4), scales=plane[:, cols], in_=source)
+
+        def widen(k, gi, j, on_scalar):
             if (k, gi) not in wide:
-                wide[k, gi] = work.tile([P, PACK, W], BF16, name="wide", bufs=2)
-            for j in js:
-                src = ss_raw[k, gi][:, j, :].bitcast(FP8)
-                dst = wide[k, gi][:, j, :]
-                if on_scalar:
-                    nc.scalar.activation(out=dst, in_=src, func=ACT.Copy, scale=sc_t[:, j : j + 1])
-                else:
-                    nc.vector.tensor_scalar(out=dst, in0=src, scalar1=sc_t[:, j : j + 1], scalar2=None, op0=ALU.mult)
-
-        def interleave(kind, k, gi, tp):
-            grp = new_grouped()
-            src = wide[k, gi] if kind == "s" else cs_raw[k, gi]
-            d = grp[:].rearrange("p (t m j) -> p m t j", t=2, j=PACK)
-            s = src[:].rearrange("p j (m t) -> p m t j", t=T)[:, :, 2 * tp : 2 * tp + 2, :]
-            if kind == "c" and k == 0:
-                nc.vector.tensor_scalar(out=d, in0=s, scalar1=-1.0, scalar2=None, op0=ALU.mult)
-            else:
-                nc.vector.tensor_copy(out=d, in_=s)
-            grouped[kind, k, gi, tp] = grp
-
-        def quant(*key):
-            c, s = new_codes("%s%d%d%d" % key)
-            nc.vector.quantize_mx(out=c[:].bitcast(FP8X4), scales=s[:], in_=grouped[key][:])
-            codes[key] = (c, s)
-
-        def transpose_x(h, c):
-            bank = psum.tile([P, 2, 2, P], F32, name=("dq", "nq")[c], bufs=2)
-            for r in range(2):
-                words = x_raw[h, c][:, r, :].bitcast(F32)
-                for u in range(2):
-                    nc.tensor.transpose(bank[:, r, u, :], words[:, u::2], ident[:])
-            xt[h, c] = bank
-
-        def copy_x(h, c, on_scalar):
-            grp = new_grouped()
-            dst = grp[:].bitcast(F32).rearrange("p (r n u) -> p r u n", r=2, u=2)
-            dst = grp[:].bitcast(F32).rearrange("p (r n u) -> p r n u", r=2, u=2)
-            src = xt[h, c][:].rearrange("p r u n -> p r n u")
+                wide[k, gi] = work.tile([P, PACK, GROUP], BF16, name="wide", bufs=2)
+            source = ss_rows[k, gi][:, j, :].bitcast(FP8)
+            scale = scale_col[:, j : j + 1]
             if on_scalar:
-                nc.scalar.copy(out=dst, in_=src)
+                nc.scalar.activation(out=wide[k, gi][:, j, :], in_=source, func=ACT.Copy, scale=scale)
             else:
-                nc.vector.tensor_copy(out=dst, in_=src)
-            grouped["x", 0, h, c] = grp
+                nc.vector.tensor_scalar(out=wide[k, gi][:, j, :], in0=source, scalar1=scale, scalar2=None, op0=ALU.mult)
 
-        def where(u):
-            return u // 8, u // 4 % 2, u // 2 % 2, u % 2
+        def interleave(kind, k, gi, pair, on_scalar=False):
+            key = (kind, k, gi)
+            if key not in grouped:
+                grouped[key] = work.tile([P, TILES * P * PACK], BF16, name="grouped", bufs=4, align_bytes=64)
+            tiles = slice(2 * pair, 2 * pair + 2)
+            rows = wide[k, gi] if kind == "ss" else cs_rows[k, gi]
+            source = rows[:].rearrange("p j (m t) -> p m t j", t=TILES)[:, :, tiles, :]
+            dest = grouped[key][:].rearrange("p (t m j) -> p m t j", t=TILES, j=PACK)[:, :, tiles, :]
+            if on_scalar:
+                nc.scalar.copy(out=dest, in_=source)
+            elif key[:2] == ("cs", 0):
+                nc.vector.tensor_scalar(out=dest, in0=source, scalar1=-1.0, scalar2=None, op0=ALU.mult)
+            else:
+                nc.vector.tensor_copy(out=dest, in_=source)
 
-        def mm1(dst, kind, k, u, start, stop):
-            gi, h, c, tp = where(u)
-            wc, ws = codes[kind, k, gi, tp]
-            xc, xs = codes["x", 0, h, c]
-            cols = slice(dst[0] * P, (dst[0] + 1) * P)
+        def quantize_weight(kind, k, gi, first_tile, tiles):
+            cols = slice(first_tile * P, (first_tile + tiles) * P)
+            source = grouped[kind, k, gi][:, PACK * cols.start : PACK * cols.stop]
+            quantize((kind, k, gi), source, GROUP, cols)
+
+        def transpose_x(q):
+            turned[q] = psum.tile([P, RTILES, 2, P], F32, name=("diff", "minus0")[q % 2], bufs=2)
+            for r in range(RTILES):
+                words = x_rows[q][:, r, :].bitcast(F32)
+                for u in range(2):
+                    nc.tensor.transpose(turned[q][:, r, u, :], words[:, u::2], ident[:])
+
+        def copy_x(q, on_scalar):
+            grouped["x", q] = work.tile([P, QROWS * PACK], BF16, name="x_grouped", bufs=2, align_bytes=64)
+            dest = grouped["x", q][:].bitcast(F32).rearrange("p (r n u) -> p r n u", r=RTILES, u=2)
+            source = turned[q][:].rearrange("p r u n -> p r n u")
+            if on_scalar:
+                nc.scalar.copy(out=dest, in_=source)
+            else:
+                nc.vector.tensor_copy(out=dest, in_=source)
+
+        def quantize_x(q):
+            quantize(("x", q), grouped["x", q][:], QROWS, slice(0, QROWS))
+
+        indicator, squares, logs, log_diff, weight = {}, {}, {}, {}, {}
+        diff, minus0, shift, blend, slope, flux = {}, {}, {}, {}, {}, {}
+
+        def split(u):
+            return u // 8, u // 2 % 4, u % 2
+
+        def channel_columns(u):
+            gi, q, pair = split(u)
+            return [(slice(i * QROWS, (i + 1) * QROWS), gi * TILES + 2 * pair + i) for i in range(2)]
+
+        def multiply(bank, u, kind, k, i, start, stop):
+            gi, q, pair = split(u)
+            words, plane = codes[kind, k, gi]
+            x_words, x_plane = codes["x", q]
+            cols = slice((2 * pair + i) * P, (2 * pair + i + 1) * P)
             nc.tensor.matmul_mx(
-                out=dst[1][:, dst[0], :],
-                lhsT=wc[:, cols].bitcast(FP8X4),
-                lhsT_scale=ws[:, cols],
-                rhs=xc[:].bitcast(FP8X4),
-                rhs_scale=xs[:],
+                out=bank[:, i * QROWS : (i + 1) * QROWS],
+                lhsT=words[:, cols].bitcast(FP8X4),
+                lhsT_scale=plane[:, cols],
+                rhs=x_words[:].bitcast(FP8X4),
+                rhs_scale=x_plane[:],
                 start=start,
                 stop=stop,
             )
 
-        s_t, e_t, l_t, z_t, w_t, dq_t, nq_t, t_t, qh_t, b_t = {}, {}, {}, {}, {}, {}, {}, {}, {}, {}
-
-        def emit_s(u, k):
-            bank = psum.tile([P, 2, C], F32, name="s", bufs=4)
+        def indicators(u, k):
+            indicator[u, k] = psum.tile([P, BANK], F32, name="indicator", bufs=4)
             for i in range(2):
-                mm1((i, bank), "s", k, u, True, True)
-            s_t[u, k] = bank
+                multiply(indicator[u, k], u, "ss", k, i, True, True)
 
-        def emit_e(u, k):
-            if u not in e_t:
-                e_t[u] = work.tile([P, K, W], F32, name="e", bufs=4)
-            src = s_t[u, k][:].rearrange("p t n -> p (t n)")
-            if [u, k] in HELP:
-                sc = work.tile([P, W], F32, name="sc", bufs=2)
-                nc.vector.tensor_copy(out=sc[:], in_=src)
-                nc.gpsimd.tensor_tensor(out=e_t[u][:, k, :], in0=sc[:], in1=sc[:], op=ALU.mult)
-            else:
-                nc.scalar.activation(out=e_t[u][:, k, :], in_=src, func=ACT.Square)
+        def square(u, k):
+            if u not in squares:
+                squares[u] = work.tile([P, K, BANK], F32, name="squares", bufs=4)
+            nc.scalar.activation(out=squares[u][:, k, :], in_=indicator[u, k][:], func=ACT.Square)
 
-        def emit_l(u):
-            l = work.tile([P, K, W], F32, name="l", bufs=4)
-            nc.scalar.activation(out=l[:], in_=e_t[u][:], func=ACT.Ln, bias=half[:, 0:1])
-            l_t[u] = l
+        def take_logs(u):
+            logs[u] = work.tile([P, K, BANK], F32, name="logs", bufs=4)
+            nc.scalar.activation(out=logs[u][:], in_=squares[u][:], func=ACT.Ln, bias=half[:, 0:1])
 
-        def emit_z(u):
-            z = work.tile([P, W], F32, name="z", bufs=11)
-            eng = nc.gpsimd if u in Z_GPSIMD else nc.vector
-            eng.tensor_tensor(out=z[:], in0=l_t[u][:, 0, :], in1=l_t[u][:, 1, :], op=ALU.subtract)
-            z_t[u] = z
+        def subtract_logs(u):
+            log_diff[u] = work.tile([P, BANK], F32, name="log_diff", bufs=10)
+            nc.vector.tensor_tensor(out=log_diff[u][:], in0=logs[u][:, 0, :], in1=logs[u][:, 1, :], op=ALU.subtract)
 
-        def emit_w(u):
-            gi, h, c, tp = where(u)
-            w = work.tile([P, W], F32, name="w", bufs=11)
+        def take_weight(u):
+            weight[u] = work.tile([P, BANK], F32, name="weight", bufs=10)
+            for cols, c in channel_columns(u):
+                nc.scalar.activation(
+                    out=weight[u][:, cols], in_=log_diff[u][:, cols], func=ACT.Sigmoid, scale=2.0, bias=log_ratio[:, c : c + 1]
+                )
+
+        def candidates(u):
+            diff[u] = psum.tile([P, BANK], F32, name="diff", bufs=2)
+            minus0[u] = psum.tile([P, BANK], F32, name="minus0", bufs=2)
             for i in range(2):
-                col = gi * T + 2 * tp + i
-                cols = slice(i * C, (i + 1) * C)
-                nc.scalar.activation(out=w[:, cols], in_=z_t[u][:, cols], func=ACT.Sigmoid, scale=2.0, bias=lnr[:, col : col + 1])
-            w_t[u] = w
-
-        def emit_dq(u):
-            dq = psum.tile([P, 2, C], F32, name="dq", bufs=2)
-            nq = psum.tile([P, 2, C], F32, name="nq", bufs=2)
+                multiply(diff[u], u, "cs", 1, i, True, False)
+                multiply(diff[u], u, "cs", 0, i, False, True)
             for i in range(2):
-                mm1((i, dq), "c", 1, u, True, False)
-                mm1((i, dq), "c", 0, u, False, True)
-            for i in range(2):
-                mm1((i, nq), "c", 0, u, True, True)
-            dq_t[u], nq_t[u] = dq, nq
+                multiply(minus0[u], u, "cs", 0, i, True, True)
 
-        def emit_t(u):
-            tt = work.tile([P, W], F32, name="tt", bufs=3)
-            nc.vector.tensor_tensor(out=tt[:], in0=dq_t[u][:].rearrange("p t n -> p (t n)"), in1=w_t[u][:], op=ALU.mult)
-            t_t[u] = tt
+        def take_shift(u):
+            shift[u] = work.tile([P, BANK], F32, name="shift", bufs=3)
+            nc.vector.tensor_tensor(out=shift[u][:], in0=diff[u][:], in1=weight[u][:], op=ALU.mult)
 
-        def emit_qh(u):
-            v, tp = u // 2, u % 2
-            if tp == 0:
-                qh_t[v] = work.tile([P, T, C], F32, name="qh", bufs=3)
-                b_t[v] = work.tile([P, T, C], F32, name="bb", bufs=3)
-            nc.vector.tensor_tensor(
-                out=qh_t[v][:, 2 * tp : 2 * tp + 2, :].rearrange("p t n -> p (t n)"),
-                in0=t_t[u][:],
-                in1=nq_t[u][:].rearrange("p t n -> p (t n)"),
-                op=ALU.subtract,
-            )
+        def take_blend(u):
+            v, pair = u // 2, u % 2
+            if pair == 0:
+                blend[v] = work.tile([P, TILES, QROWS], F32, name="blend", bufs=3)
+                slope[v] = work.tile([P, TILES, QROWS], F32, name="slope", bufs=3)
+            dest = blend[v][:, 2 * pair : 2 * pair + 2, :].rearrange("p t n -> p (t n)")
+            nc.vector.tensor_tensor(out=dest, in0=shift[u][:], in1=minus0[u][:], op=ALU.subtract)
 
-        def emit_b(u):
-            gi, h, c, tp = where(u)
-            for i in range(2):
-                t = 2 * tp + i
-                col = gi * T + t
-                dst, src = b_t[u // 2][:, t, :], qh_t[u // 2][:, t, :]
-                if B_ENG[u] == "S":
-                    nc.scalar.activation(out=dst, in_=src, func=ACT.Identity, scale=gh[:, col : col + 1], bias=gf[:, col : col + 1])
+        def take_slope(u):
+            for i, (cols, c) in enumerate(channel_columns(u)):
+                t = 2 * (u % 2) + i
+                dest, source = slope[u // 2][:, t, :], blend[u // 2][:, t, :]
+                if u in SLOPE_ON_SCALAR:
+                    nc.scalar.activation(out=dest, in_=source, func=ACT.Identity, scale=half_gain[:, c : c + 1], bias=gain[:, c : c + 1])
                 else:
-                    eng = nc.gpsimd if B_ENG[u] == "G" else nc.vector
-                    eng.tensor_scalar(out=dst, in0=src, scalar1=gh[:, col : col + 1], scalar2=gf[:, col : col + 1], op0=ALU.mult, op1=ALU.add)
+                    nc.vector.tensor_scalar(
+                        out=dest, in0=source, scalar1=half_gain[:, c : c + 1], scalar2=gain[:, c : c + 1], op0=ALU.mult, op1=ALU.add
+                    )
 
-        def emit_pg(u, cols):
-            v = u // 2
-            if v not in pg_t:
-                pg_t[v] = work.tile([P, C, T], BF16, name="pg", bufs=3, align_bytes=64)
-                codes["p", v] = new_codes("p%d" % v)
+        def take_flux(v, rows):
+            if v not in flux:
+                flux[v] = work.tile([P, QROWS, TILES], BF16, name="flux", bufs=3, align_bytes=64)
             nc.vector.tensor_tensor(
-                out=pg_t[v][:, cols, :].rearrange("p (c i) t -> p c t i", i=4),
-                in0=b_t[v][:, :, cols].rearrange("p t (c i) -> p c t i", i=4),
-                in1=qh_t[v][:, :, cols].rearrange("p t (c i) -> p c t i", i=4),
+                out=flux[v][:, rows, :].rearrange("p (c i) t -> p c t i", i=4),
+                in0=slope[v][:, :, rows].rearrange("p t (c i) -> p c t i", i=4),
+                in1=blend[v][:, :, rows].rearrange("p t (c i) -> p c t i", i=4),
                 op=ALU.mult,
             )
 
-        def emit_qp(u, cols):
-            v = u // 2
-            c, s = codes["p", v]
-            nc.vector.quantize_mx(out=c[:, cols].bitcast(FP8X4), scales=s[:, cols], in_=pg_t[v][:, cols, :].rearrange("p n t -> p (n t)"))
+        def quantize_flux(v, rows):
+            quantize(("pg", v), flux[v][:, rows, :].rearrange("p n t -> p (n t)"), QROWS, rows)
 
-        outs = {}
-        pg_t = {}
+        result = {}
 
-        def emit_m(u, r):
-            v = u // 2
-            bank = psum.tile([P, W], F32, name="s", bufs=4)
+        def second_stage(q, r, gi):
+            if gi == 0:
+                result[q, r] = psum.tile([P, D], F32, name="indicator", bufs=4)
+            words, plane = codes["pg", QUARTERS * gi + q]
             cols = slice(r * P, (r + 1) * P)
-            for gi in range(G):
-                c, s = codes["p", v - 4 + 4 * gi]
-                nc.tensor.matmul_mx(
-                    out=bank[:],
-                    lhsT=c[:, cols].bitcast(FP8X4),
-                    lhsT_scale=s[:, cols],
-                    rhs=dvw[:, gi, :].bitcast(FP4X4),
-                    rhs_scale=dvs[:, gi, :],
-                    start=(gi == 0),
-                    stop=(gi == G - 1),
-                )
-            outs[u, r] = bank
+            nc.tensor.matmul_mx(
+                out=result[q, r][:],
+                lhsT=words[:, cols].bitcast(FP8X4),
+                lhsT_scale=plane[:, cols],
+                rhs=dv_codes[:, gi, :].bitcast(FP4X4),
+                rhs_scale=dv_plane[:, gi, :],
+                start=(gi == 0),
+                stop=(gi == GROUPS - 1),
+            )
 
-        def emit_o(u, r):
-            gi, h, c, tp = where(u)
-            o = work.tile([P, D], F32, name="o", bufs=4)
-            if [u, r] in OUT_SCALAR:
-                nc.scalar.copy(out=o[:], in_=outs[u, r][:])
+        def store(q, r, on_scalar):
+            rows = work.tile([P, D], F32, name="out_rows", bufs=8)
+            if on_scalar:
+                nc.scalar.copy(out=rows[:], in_=result[q, r][:])
             else:
-                nc.vector.tensor_copy(out=o[:], in_=outs[u, r][:])
-            nc.sync.dma_start(out=out[h * W : (h + 1) * W, :].rearrange("(p r) d -> p r d", r=4)[:, 2 * c + r, :], in_=o[:])
+                nc.vector.tensor_copy(out=rows[:], in_=result[q, r][:])
+            nc.sync.dma_start(out=out[q * QROWS : (q + 1) * QROWS, :].rearrange("(p r) d -> p r d", r=RTILES)[:, r, :], in_=rows[:])
 
-        lg = [const.tile([P, G * T], F32, name="lg%d" % k) for k in range(K)]
-        lnr = const.tile([P, G * T], F32, name="lnr")
-        gf = const.tile([P, G * T], F32, name="gf")
-        gh = const.tile([P, G * T], F32, name="gh")
+        def row_tile(r):
+            return slice(r * P, (r + 1) * P)
 
-        ALL = [0, 1, 2, 3]
-        transpose_x(0, 0)
-        widen(0, 0, [0], False)
-        widen(0, 0, [1], False)
-        widen(0, 0, [2], False)
-        widen(0, 0, [3], False)
-        copy_x(0, 0, True)
-        interleave("s", 0, 0, 0)
-        widen(1, 0, [2], True)
-        widen(1, 0, [3], True)
-        quant("s", 0, 0, 0)
-        interleave("s", 0, 0, 1)
-        quant("x", 0, 0, 0)
-        emit_s(0, 0)
-        emit_e(0, 0)
-        widen(1, 0, [0], False)
-        widen(1, 0, [1], False)
-        quant("s", 0, 0, 1)
-        emit_s(1, 0)
-        emit_e(1, 0)
-        interleave("s", 1, 0, 0)
-        quant("s", 1, 0, 0)
-        emit_s(0, 1)
-        emit_e(0, 1)
-        transpose_x(0, 1)
-        copy_x(0, 1, True)
-        interleave("s", 1, 0, 1)
-        quant("s", 1, 0, 1)
-        emit_s(1, 1)
-        quant("x", 0, 0, 1)
-        HEAD_E = [(0, 0), (1, 0), (0, 1)]
-        def channel_constants():
+        def flux_step(step):
+            for u in (step, step + 1):
+                if u < UNITS and u not in diff:
+                    candidates(u)
+            if step < UNITS:
+                take_shift(step)
+            if 0 <= step - 2 < UNITS:
+                take_slope(step - 2)
+            if 0 <= step - 1 < UNITS:
+                take_blend(step - 1)
+            last = UNITS // 2 - 1
+            if (step - 3) % 2 == 1 and 0 <= (step - 3) // 2 < last:
+                take_flux((step - 3) // 2, slice(0, QROWS))
+            if step - 3 == UNITS - 1:
+                for r in range(RTILES):
+                    take_flux(last, row_tile(r))
+                for r in range(RTILES):
+                    second_stage(QUARTERS - 1, r, 0)
+                for r in range(RTILES):
+                    quantize_flux(last, row_tile(r))
+                    second_stage(QUARTERS - 1, r, 1)
+            if (step - 4) % 2 == 1 and 0 <= (step - 4) // 2 < last:
+                v = (step - 4) // 2
+                quantize_flux(v, slice(0, QROWS))
+                if v >= QUARTERS:
+                    for gi in range(GROUPS):
+                        for r in range(RTILES):
+                            second_stage(v - QUARTERS, r, gi)
+            if (step - 5) % 2 == 1 and QUARTERS <= (step - 5) // 2 <= last:
+                q = (step - 5) // 2 - QUARTERS
+                for r in range(RTILES):
+                    store(q, r, (q, r) != (QUARTERS - 1, 0))
+
+        keep_busy("indicator", 4, 6)
+        transpose_x(0)
+        widen(0, 0, 0, True)
+        for j in (3, 2, 1):
+            widen(0, 0, j, False)
+        interleave("ss", 0, 0, 0)
+        copy_x(0, True)
+        widen(1, 0, 3, False)
+        interleave("ss", 0, 0, 1)
+        for j in (1, 2):
+            widen(1, 0, j, True)
+        quantize_weight("ss", 0, 0, 0, 2)
+        widen(1, 0, 0, False)
+        quantize_x(0)
+        quantize_weight("ss", 0, 0, 2, 2)
+        interleave("ss", 1, 0, 0)
+        interleave("ss", 1, 0, 1, True)
+        indicators(0, 0)
+        quantize_weight("ss", 1, 0, 0, 2)
+        transpose_x(1)
+        indicators(1, 0)
+        square(0, 0)
+        square(1, 0)
+        indicators(0, 1)
+        quantize_weight("ss", 1, 0, 2, 2)
+        indicators(1, 1)
+        copy_x(1, False)
+        quantize_x(1)
+        square(0, 1)
+        square(1, 1)
+
+        prep = []
+        for q in (2, 3):
+            prep.append([(transpose_x, (q,)), (copy_x, (q, False))])
+        for q in (2, 3):
+            prep.append([(quantize_x, (q,))])
+        for k in range(K):
+            prep.append([(widen, (k, 1, j, False)) for j in range(PACK)])
+        for kind, gi in (("ss", 1), ("cs", 0), ("cs", 1)):
+            for pair in range(2):
+                for k in range(K):
+                    prep.append([(interleave, (kind, k, gi, pair))])
             for k in range(K):
-                nc.scalar.activation(out=lg[k][:], in_=gam_t[k][:].rearrange("p g t -> p (g t)"), func=ACT.Ln)
-            nc.gpsimd.tensor_tensor(out=lnr[:], in0=lg[1][:], in1=lg[0][:], op=ALU.subtract)
-            nc.gpsimd.tensor_copy(out=gf[:], in_=g_t[:].rearrange("p g t -> p (g t)"))
-            nc.gpsimd.tensor_scalar(out=gh[:], in0=gf[:], scalar1=0.5, scalar2=0.0, op0=ALU.mult, op1=ALU.add)
+                prep.append([(quantize_weight, (kind, k, gi, 0, TILES))])
 
-        items = list(PREP_ITEMS)
-
-        def prep(n):
-            for it in items[:n]:
-                if it[0] == "x":
-                    transpose_x(it[1], it[2])
-                    copy_x(it[1], it[2], False)
-                elif it[0] == "qx":
-                    quant("x", 0, it[1], it[2])
-                elif it[0] == "wd":
-                    widen(it[1], it[2], ALL, False)
-                elif it[0] == "il":
-                    interleave(it[1], it[2], it[3], it[4])
-                else:
-                    quant(it[1], it[2], it[3], it[4])
-            del_n = min(n, len(items))
-            items[:] = items[del_n:]
-
-        state = {"v": 0}
-
-        def dq(v):
-            if v < N and v not in dq_t:
-                emit_dq(v)
-
-        def flux():
-            v = state["v"]
-            dq(v)
-            dq(v + 1)
-            if v < N:
-                emit_t(v)
-            if 2 <= v <= N + 1:
-                emit_b(v - 2)
-            if 1 <= v <= N:
-                emit_qh(v - 1)
-            w = v - 2 - LAG
-            if 0 <= w < N - 1 and w % 2 == 1:
-                emit_pg(w, slice(0, C))
-            if w == N - 1:
-                for r in range(2):
-                    emit_pg(w, slice(r * P, (r + 1) * P))
-                for r in range(2):
-                    emit_qp(w, slice(r * P, (r + 1) * P))
-                    emit_m(w, r)
-            w = v - 3 - LAG
-            if 0 <= w < N - 1 and w % 2 == 1:
-                emit_qp(w, slice(0, C))
-                if w >= 8:
-                    for r in range(2):
-                        emit_m(w, r)
-            w = v - 4 - LAG
-            if 8 <= w < N and w % 2 == 1:
-                for r in range(2):
-                    emit_o(w, r)
-            state["v"] = v + 1
-
-        def s(u):
-            for k in range(K):
-                if u < N and (u, k) not in s_t:
-                    emit_s(u, k)
-
-        done = []
-
-        def e(u):
-            for k in range(K):
-                if u < N and (u, k) not in HEAD_E and (u, k) not in done:
-                    done.append((u, k))
-                    emit_e(u, k)
-
-        u = 0
-        for n in CHUNKS:
-            for i in range(u, u + n):
-                prep(PREP[i])
-                s(i)
-                s(i + 1)
-                e(i)
-                e(i + 1)
-                s(i + 2)
-                emit_l(i)
-                if i == 6:
+        steps = 0
+        for chunk, count in enumerate(CHUNKS):
+            first = sum(CHUNKS[:chunk])
+            for u in range(first, first + count):
+                for item in prep[: PREP_FIRST if u == 0 else PREP_EACH]:
+                    for function, arguments in item:
+                        function(*arguments)
+                prep = prep[PREP_FIRST if u == 0 else PREP_EACH :]
+                if 1 <= u < UNITS - 1:
+                    for k in range(K):
+                        square(u + 1, k)
+                if u + 2 < UNITS:
+                    for k in range(K):
+                        indicators(u + 2, k)
+                if chunk == 0 and u >= 2:
+                    keep_busy("minus0", 2, 1)
+                take_logs(u)
+                if u == 6:
                     channel_constants()
-                if i > u:
-                    emit_z(i - 1)
-                for _ in range(RATE[i]):
-                    flux()
-            emit_z(u + n - 1)
-            for i in range(u, u + n):
-                emit_w(i)
-            for _ in range(sum(WRATE[u : u + n])):
-                flux()
-            u += n
-        prep(99)
-        while state["v"] < N + 5 + LAG:
-            flux()
+                if u > first:
+                    subtract_logs(u - 1)
+                if chunk > 0:
+                    flux_step(steps)
+                    steps += 1
+            subtract_logs(first + count - 1)
+            for u in range(first, first + count):
+                take_weight(u)
+            for _ in range(FLUX_BEHIND[chunk]):
+                flux_step(steps)
+                steps += 1
+        while steps < UNITS + 5:
+            flux_step(steps)
+            steps += 1

from contextlib import ExitStack

import concourse.mybir as mybir
from concourse.masks import make_identity

F32 = mybir.dt.float32
BF16 = mybir.dt.bfloat16
I32 = mybir.dt.int32
U32 = mybir.dt.uint32
U8 = mybir.dt.uint8
FP8 = mybir.dt.float8_e4m3fn
FP8X4 = mybir.dt.float8_e4m3fn_x4
FP4X4 = mybir.dt.float4_e2m1fn_x4

ACT = mybir.ActivationFunctionType
ALU = mybir.AluOpType

B, D, F, K = 1024, 512, 1024, 2
FLOPS = 2 * B * D * F * 2 * K + 2 * B * F * D

P = 128
PACK = 4
GROUP = P * PACK
GROUPS = F // GROUP
TILES = 4
QROWS = 256
QUARTERS = B // QROWS
RTILES = QROWS // P
BANK = 512

UNITS = GROUPS * QUARTERS * TILES // 2

CHUNKS = (9, 5, 2)
FLUX_BEHIND = (4, 2, 0)
PREP_FIRST, PREP_EACH = 6, 3
SLOPE_ON_SCALAR = range(9, 15)


def tile_learnedstencilwenostep_w4_kernel(tc, x, cs, ss_bytes, ss_scale, gamma, g, dv_words, dv_scales, out):
    nc = tc.nc
    with ExitStack() as ctx:
        const = ctx.enter_context(tc.tile_pool(name="const", bufs=1))
        work = ctx.enter_context(tc.tile_pool(name="work", bufs=2))
        psum = ctx.enter_context(tc.psum_pool(name="psum", bufs=1))
        ctx.enter_context(tc.manual_schedule())

        scale_col = const.tile([P, PACK], F32, name="scale_col")
        nc.scalar.dma_start(out=scale_col[:], in_=ss_scale.rearrange("o (p j) u -> p (o j u)", j=PACK))

        ss_rows, cs_rows, x_rows = {}, {}, {}

        def load_weight(rows, name, source, dtype, k, gi):
            rows[k, gi] = const.tile([P, PACK, GROUP], dtype, name="%s%d%d" % (name, k, gi))
            cols = slice(gi * GROUP, (gi + 1) * GROUP)
            nc.sync.dma_start(out=rows[k, gi][:], in_=source[k].rearrange("(p j) f -> p j f", j=PACK)[:, :, cols])

        def load_x(q):
            x_rows[q] = const.tile([P, RTILES, D], BF16, name="x_rows%d" % q)
            nc.sync.dma_start(out=x_rows[q][:], in_=x[q * QROWS : (q + 1) * QROWS, :].rearrange("(p r) d -> p r d", r=RTILES))

        def load_channels(vector, name):
            tile = const.tile([P, GROUPS, TILES], BF16, name=name)
            nc.sync.dma_start(out=tile[:], in_=vector.rearrange("(g p t) -> p g t", g=GROUPS, t=TILES))
            return tile[:].rearrange("p g t -> p (g t)")

        load_weight(ss_rows, "ss_rows", ss_bytes, U8, 0, 0)
        load_x(0)
        load_weight(ss_rows, "ss_rows", ss_bytes, U8, 1, 0)
        for q in range(1, QUARTERS):
            load_x(q)
        for k in range(K):
            load_weight(ss_rows, "ss_rows", ss_bytes, U8, k, 1)
        for k in range(K):
            load_weight(cs_rows, "cs_rows", cs, BF16, k, 0)
        gamma_bf = [load_channels(gamma[k, :], "gamma_bf%d" % k) for k in range(K)]
        gain_bf = load_channels(g, "gain_bf")
        for k in range(K):
            load_weight(cs_rows, "cs_rows", cs, BF16, k, 1)
        dv_codes = const.tile([P, GROUPS, 2 * D], U8, name="dv_codes", align_bytes=64)
        nc.sync.dma_start(out=dv_codes[:], in_=dv_words.rearrange("g p c -> p g c"))
        dv_plane = const.tile([P, GROUPS, D], U8, name="dv_plane", align_bytes=64)
        nc.gpsimd.memset(dv_plane[:].rearrange("p g d -> p (g d)").bitcast(I32), 0)
        for quadrant in range(4):
            nc.sync.dma_start(
                out=dv_plane[32 * quadrant : 32 * quadrant + 4, :, :].bitcast(I32),
                in_=dv_scales[:, 4 * quadrant : 4 * quadrant + 4, :].rearrange("g r d -> r g d").bitcast(I32),
            )

        half = const.tile([P, 1], F32, name="half")
        nc.gpsimd.memset(half[:], 0.5)
        ident = const.tile([P, P], F32, name="ident")
        make_identity(nc, ident[:])
        zeros = const.tile([P, BANK], BF16, name="zeros")
        nc.vector.memset(zeros[:], 0.0)
        unused = const.tile([P, 1], F32, name="unused")
        nc.scalar.activation(out=unused[:], in_=half[:], func=ACT.Ln, bias=half[:, 0:1])

        log_gamma = [const.tile([P, GROUPS * TILES], F32, name="log_gamma%d" % k) for k in range(K)]
        log_ratio = const.tile([P, GROUPS * TILES], F32, name="log_ratio")
        gain = const.tile([P, GROUPS * TILES], F32, name="gain")
        half_gain = const.tile([P, GROUPS * TILES], F32, name="half_gain")

        def channel_constants():
            for k in range(K):
                nc.scalar.activation(out=log_gamma[k][:], in_=gamma_bf[k], func=ACT.Ln)
            nc.gpsimd.tensor_tensor(out=log_ratio[:], in0=log_gamma[1][:], in1=log_gamma[0][:], op=ALU.subtract)
            nc.gpsimd.tensor_copy(out=gain[:], in_=gain_bf)
            nc.gpsimd.tensor_scalar(out=half_gain[:], in0=gain[:], scalar1=0.5, scalar2=0.0, op0=ALU.mult, op1=ALU.add)

        def keep_busy(tag, bufs, passes):
            bank = psum.tile([P, BANK], F32, name=tag, bufs=bufs)
            for _ in range(passes):
                nc.tensor.matmul(out=bank[:], lhsT=zeros[:, 0:P], rhs=zeros[:], start=True, stop=True)

        wide, grouped, codes, turned = {}, {}, {}, {}

        def new_codes(key, columns):
            name = "_".join([str(part) for part in key])
            words = const.tile([P, columns], U32, name="words_" + name, align_bytes=64)
            plane = const.tile([P, columns], U8, name="plane_" + name, align_bytes=64)
            codes[key] = (words, plane)

        def quantize(key, source, columns, cols):
            if key not in codes:
                new_codes(key, columns)
            words, plane = codes[key]
            nc.vector.quantize_mx(out=words[:, cols].bitcast(FP8X4), scales=plane[:, cols], in_=source)

        def widen(k, gi, j, on_scalar):
            if (k, gi) not in wide:
                wide[k, gi] = work.tile([P, PACK, GROUP], BF16, name="wide", bufs=2)
            source = ss_rows[k, gi][:, j, :].bitcast(FP8)
            scale = scale_col[:, j : j + 1]
            if on_scalar:
                nc.scalar.activation(out=wide[k, gi][:, j, :], in_=source, func=ACT.Copy, scale=scale)
            else:
                nc.vector.tensor_scalar(out=wide[k, gi][:, j, :], in0=source, scalar1=scale, scalar2=None, op0=ALU.mult)

        def interleave(kind, k, gi, pair, on_scalar=False):
            key = (kind, k, gi)
            if key not in grouped:
                grouped[key] = work.tile([P, TILES * P * PACK], BF16, name="grouped", bufs=4, align_bytes=64)
            tiles = slice(2 * pair, 2 * pair + 2)
            rows = wide[k, gi] if kind == "ss" else cs_rows[k, gi]
            source = rows[:].rearrange("p j (m t) -> p m t j", t=TILES)[:, :, tiles, :]
            dest = grouped[key][:].rearrange("p (t m j) -> p m t j", t=TILES, j=PACK)[:, :, tiles, :]
            if on_scalar:
                nc.scalar.copy(out=dest, in_=source)
            elif key[:2] == ("cs", 0):
                nc.vector.tensor_scalar(out=dest, in0=source, scalar1=-1.0, scalar2=None, op0=ALU.mult)
            else:
                nc.vector.tensor_copy(out=dest, in_=source)

        def quantize_weight(kind, k, gi, first_tile, tiles):
            cols = slice(first_tile * P, (first_tile + tiles) * P)
            source = grouped[kind, k, gi][:, PACK * cols.start : PACK * cols.stop]
            quantize((kind, k, gi), source, GROUP, cols)

        def transpose_x(q):
            turned[q] = psum.tile([P, RTILES, 2, P], F32, name=("diff", "minus0")[q % 2], bufs=2)
            for r in range(RTILES):
                words = x_rows[q][:, r, :].bitcast(F32)
                for u in range(2):
                    nc.tensor.transpose(turned[q][:, r, u, :], words[:, u::2], ident[:])

        def copy_x(q, on_scalar):
            grouped["x", q] = work.tile([P, QROWS * PACK], BF16, name="x_grouped", bufs=2, align_bytes=64)
            dest = grouped["x", q][:].bitcast(F32).rearrange("p (r n u) -> p r n u", r=RTILES, u=2)
            source = turned[q][:].rearrange("p r u n -> p r n u")
            if on_scalar:
                nc.scalar.copy(out=dest, in_=source)
            else:
                nc.vector.tensor_copy(out=dest, in_=source)

        def quantize_x(q):
            quantize(("x", q), grouped["x", q][:], QROWS, slice(0, QROWS))

        indicator, squares, logs, log_diff, weight = {}, {}, {}, {}, {}
        diff, minus0, shift, blend, slope, flux = {}, {}, {}, {}, {}, {}

        def split(u):
            return u // 8, u // 2 % 4, u % 2

        def channel_columns(u):
            gi, q, pair = split(u)
            return [(slice(i * QROWS, (i + 1) * QROWS), gi * TILES + 2 * pair + i) for i in range(2)]

        def multiply(bank, u, kind, k, i, start, stop):
            gi, q, pair = split(u)
            words, plane = codes[kind, k, gi]
            x_words, x_plane = codes["x", q]
            cols = slice((2 * pair + i) * P, (2 * pair + i + 1) * P)
            nc.tensor.matmul_mx(
                out=bank[:, i * QROWS : (i + 1) * QROWS],
                lhsT=words[:, cols].bitcast(FP8X4),
                lhsT_scale=plane[:, cols],
                rhs=x_words[:].bitcast(FP8X4),
                rhs_scale=x_plane[:],
                start=start,
                stop=stop,
            )

        def indicators(u, k):
            indicator[u, k] = psum.tile([P, BANK], F32, name="indicator", bufs=4)
            for i in range(2):
                multiply(indicator[u, k], u, "ss", k, i, True, True)

        def square(u, k):
            if u not in squares:
                squares[u] = work.tile([P, K, BANK], F32, name="squares", bufs=4)
            nc.scalar.activation(out=squares[u][:, k, :], in_=indicator[u, k][:], func=ACT.Square)

        def take_logs(u):
            logs[u] = work.tile([P, K, BANK], F32, name="logs", bufs=4)
            nc.scalar.activation(out=logs[u][:], in_=squares[u][:], func=ACT.Ln, bias=half[:, 0:1])

        def subtract_logs(u):
            log_diff[u] = work.tile([P, BANK], F32, name="log_diff", bufs=10)
            nc.vector.tensor_tensor(out=log_diff[u][:], in0=logs[u][:, 0, :], in1=logs[u][:, 1, :], op=ALU.subtract)

        def take_weight(u):
            weight[u] = work.tile([P, BANK], F32, name="weight", bufs=10)
            for cols, c in channel_columns(u):
                nc.scalar.activation(
                    out=weight[u][:, cols], in_=log_diff[u][:, cols], func=ACT.Sigmoid, scale=2.0, bias=log_ratio[:, c : c + 1]
                )

        def candidates(u):
            diff[u] = psum.tile([P, BANK], F32, name="diff", bufs=2)
            minus0[u] = psum.tile([P, BANK], F32, name="minus0", bufs=2)
            for i in range(2):
                multiply(diff[u], u, "cs", 1, i, True, False)
                multiply(diff[u], u, "cs", 0, i, False, True)
            for i in range(2):
                multiply(minus0[u], u, "cs", 0, i, True, True)

        def take_shift(u):
            shift[u] = work.tile([P, BANK], F32, name="shift", bufs=3)
            nc.vector.tensor_tensor(out=shift[u][:], in0=diff[u][:], in1=weight[u][:], op=ALU.mult)

        def take_blend(u):
            v, pair = u // 2, u % 2
            if pair == 0:
                blend[v] = work.tile([P, TILES, QROWS], F32, name="blend", bufs=3)
                slope[v] = work.tile([P, TILES, QROWS], F32, name="slope", bufs=3)
            dest = blend[v][:, 2 * pair : 2 * pair + 2, :].rearrange("p t n -> p (t n)")
            nc.vector.tensor_tensor(out=dest, in0=shift[u][:], in1=minus0[u][:], op=ALU.subtract)

        def take_slope(u):
            for i, (cols, c) in enumerate(channel_columns(u)):
                t = 2 * (u % 2) + i
                dest, source = slope[u // 2][:, t, :], blend[u // 2][:, t, :]
                if u in SLOPE_ON_SCALAR:
                    nc.scalar.activation(out=dest, in_=source, func=ACT.Identity, scale=half_gain[:, c : c + 1], bias=gain[:, c : c + 1])
                else:
                    nc.vector.tensor_scalar(
                        out=dest, in0=source, scalar1=half_gain[:, c : c + 1], scalar2=gain[:, c : c + 1], op0=ALU.mult, op1=ALU.add
                    )

        def take_flux(v, rows):
            if v not in flux:
                flux[v] = work.tile([P, QROWS, TILES], BF16, name="flux", bufs=3, align_bytes=64)
            nc.vector.tensor_tensor(
                out=flux[v][:, rows, :].rearrange("p (c i) t -> p c t i", i=4),
                in0=slope[v][:, :, rows].rearrange("p t (c i) -> p c t i", i=4),
                in1=blend[v][:, :, rows].rearrange("p t (c i) -> p c t i", i=4),
                op=ALU.mult,
            )

        def quantize_flux(v, rows):
            quantize(("pg", v), flux[v][:, rows, :].rearrange("p n t -> p (n t)"), QROWS, rows)

        result = {}

        def second_stage(q, r, gi):
            if gi == 0:
                result[q, r] = psum.tile([P, D], F32, name="indicator", bufs=4)
            words, plane = codes["pg", QUARTERS * gi + q]
            cols = slice(r * P, (r + 1) * P)
            nc.tensor.matmul_mx(
                out=result[q, r][:],
                lhsT=words[:, cols].bitcast(FP8X4),
                lhsT_scale=plane[:, cols],
                rhs=dv_codes[:, gi, :].bitcast(FP4X4),
                rhs_scale=dv_plane[:, gi, :],
                start=(gi == 0),
                stop=(gi == GROUPS - 1),
            )

        def store(q, r, on_scalar):
            rows = work.tile([P, D], F32, name="out_rows", bufs=8)
            if on_scalar:
                nc.scalar.copy(out=rows[:], in_=result[q, r][:])
            else:
                nc.vector.tensor_copy(out=rows[:], in_=result[q, r][:])
            nc.sync.dma_start(out=out[q * QROWS : (q + 1) * QROWS, :].rearrange("(p r) d -> p r d", r=RTILES)[:, r, :], in_=rows[:])

        def row_tile(r):
            return slice(r * P, (r + 1) * P)

        def flux_step(step):
            for u in (step, step + 1):
                if u < UNITS and u not in diff:
                    candidates(u)
            if step < UNITS:
                take_shift(step)
            if 0 <= step - 2 < UNITS:
                take_slope(step - 2)
            if 0 <= step - 1 < UNITS:
                take_blend(step - 1)
            last = UNITS // 2 - 1
            if (step - 3) % 2 == 1 and 0 <= (step - 3) // 2 < last:
                take_flux((step - 3) // 2, slice(0, QROWS))
            if step - 3 == UNITS - 1:
                for r in range(RTILES):
                    take_flux(last, row_tile(r))
                for r in range(RTILES):
                    second_stage(QUARTERS - 1, r, 0)
                for r in range(RTILES):
                    quantize_flux(last, row_tile(r))
                    second_stage(QUARTERS - 1, r, 1)
            if (step - 4) % 2 == 1 and 0 <= (step - 4) // 2 < last:
                v = (step - 4) // 2
                quantize_flux(v, slice(0, QROWS))
                if v >= QUARTERS:
                    for gi in range(GROUPS):
                        for r in range(RTILES):
                            second_stage(v - QUARTERS, r, gi)
            if (step - 5) % 2 == 1 and QUARTERS <= (step - 5) // 2 <= last:
                q = (step - 5) // 2 - QUARTERS
                for r in range(RTILES):
                    store(q, r, (q, r) != (QUARTERS - 1, 0))

        keep_busy("indicator", 4, 6)
        transpose_x(0)
        widen(0, 0, 0, True)
        for j in (3, 2, 1):
            widen(0, 0, j, False)
        interleave("ss", 0, 0, 0)
        copy_x(0, True)
        widen(1, 0, 3, False)
        interleave("ss", 0, 0, 1)
        for j in (1, 2):
            widen(1, 0, j, True)
        quantize_weight("ss", 0, 0, 0, 2)
        widen(1, 0, 0, False)
        quantize_x(0)
        quantize_weight("ss", 0, 0, 2, 2)
        interleave("ss", 1, 0, 0)
        interleave("ss", 1, 0, 1, True)
        indicators(0, 0)
        quantize_weight("ss", 1, 0, 0, 2)
        transpose_x(1)
        indicators(1, 0)
        square(0, 0)
        square(1, 0)
        indicators(0, 1)
        quantize_weight("ss", 1, 0, 2, 2)
        indicators(1, 1)
        copy_x(1, False)
        quantize_x(1)
        square(0, 1)
        square(1, 1)

        prep = []
        for q in (2, 3):
            prep.append([(transpose_x, (q,)), (copy_x, (q, False))])
        for q in (2, 3):
            prep.append([(quantize_x, (q,))])
        for k in range(K):
            prep.append([(widen, (k, 1, j, False)) for j in range(PACK)])
        for kind, gi in (("ss", 1), ("cs", 0), ("cs", 1)):
            for pair in range(2):
                for k in range(K):
                    prep.append([(interleave, (kind, k, gi, pair))])
            for k in range(K):
                prep.append([(quantize_weight, (kind, k, gi, 0, TILES))])

        steps = 0
        for chunk, count in enumerate(CHUNKS):
            first = sum(CHUNKS[:chunk])
            for u in range(first, first + count):
                for item in prep[: PREP_FIRST if u == 0 else PREP_EACH]:
                    for function, arguments in item:
                        function(*arguments)
                prep = prep[PREP_FIRST if u == 0 else PREP_EACH :]
                if 1 <= u < UNITS - 1:
                    for k in range(K):
                        square(u + 1, k)
                if u + 2 < UNITS:
                    for k in range(K):
                        indicators(u + 2, k)
                if chunk == 0 and u >= 2:
                    keep_busy("minus0", 2, 1)
                take_logs(u)
                if u == 6:
                    channel_constants()
                if u > first:
                    subtract_logs(u - 1)
                if chunk > 0:
                    flux_step(steps)
                    steps += 1
            subtract_logs(first + count - 1)
            for u in range(first, first + count):
                take_weight(u)
            for _ in range(FLUX_BEHIND[chunk]):
                flux_step(steps)
                steps += 1
        while steps < UNITS + 5:
            flux_step(steps)
            steps += 1
